import numpy as np
import ml_dtypes


def mxq(x, axis, fmt="e4m3"):
    dtype, down = {"e4m3": (ml_dtypes.float8_e4m3fn, 7), "e5m2": (ml_dtypes.float8_e5m2, 14)}[fmt]
    v = np.moveaxis(np.asarray(x, np.float32).astype(ml_dtypes.bfloat16).astype(np.float64), axis, -1)
    blocks = v.reshape(v.shape[:-1] + (-1, 32))
    amax = np.abs(blocks).max(-1, keepdims=True)
    byte = np.maximum(np.where(amax > 0, np.frexp(amax)[1] - 1 + 127, 0) - down, 1)
    scale = np.exp2(byte - 127.0)
    codes = (blocks / scale).astype(np.float32).astype(dtype).astype(np.float64)
    return np.moveaxis((codes * scale).reshape(v.shape), -1, axis)


WIDE = False


def mx_kscale(k):
    if not WIDE:
        return np.ones(k)
    levels = np.array([10, -10, 5, -5, 0])
    if k % 512:
        return np.exp2(np.random.permutation(np.resize(levels, k // 32))).repeat(32)
    a = np.empty((k // 512, 16))
    for p in range(k // 512):
        a[p, :8] = np.random.permutation(np.resize(levels, 8))
        for g in range(8):
            far = levels[np.abs(levels - a[p, g]) >= 10]
            a[p, g + 8] = far[np.random.randint(len(far))]
    return np.exp2(a.ravel()).repeat(32)


BF16 = ml_dtypes.bfloat16


def bf(x):
    return np.asarray(x, np.float32).astype(BF16)


def f64(x):
    return np.asarray(x).astype(np.float64)


E2M1 = np.array([0.0, 0.5, 1.0, 1.5, 2.0, 3.0, 4.0, 6.0, -0.0, -0.5, -1.0, -1.5, -2.0, -3.0, -4.0, -6.0])


def pack_weight(w, fmt):
    k, n = w.shape
    w = f64(bf(w)).reshape(k // 32, 32, n)
    amax = np.abs(w).max(1)
    if fmt == "e4m3":
        byte = np.frexp(amax)[1] - 1 + 127 - 7
    else:
        mant, ex = np.frexp(amax / 6.0)
        byte = np.where(mant > 0.5, ex, ex - 1) + 127
    byte = np.clip(np.where(amax > 0, byte, 1), 1, 254)
    scaled = (w * np.exp2(127.0 - byte)[:, None, :]).reshape(k, n).astype(np.float32)
    by_word = np.ascontiguousarray(scaled.reshape(k // 512, 128, 4, n).transpose(0, 1, 3, 2))
    if fmt == "e4m3":
        words = by_word.astype(ml_dtypes.float8_e4m3fn).view(np.uint8)
    else:
        c = by_word.astype(ml_dtypes.float4_e2m1fn).view(np.uint8) & 0xF
        words = c[..., 0::2] | (c[..., 1::2] << 4)
    return np.ascontiguousarray(words), np.ascontiguousarray(byte.astype(np.uint8).reshape(k // 512, 16, n))


def unpack_weight(words, scales, fmt):
    g, p, n, _ = words.shape
    if fmt == "e4m3":
        vals = np.ascontiguousarray(words).view(ml_dtypes.float8_e4m3fn).astype(np.float64)
    else:
        nib = np.empty((g, p, n, 4), np.uint8)
        nib[..., 0::2] = words & 0xF
        nib[..., 1::2] = words >> 4
        vals = E2M1[nib]
    vals = vals * np.repeat(np.exp2(scales.astype(np.float64) - 127.0), 8, axis=1)[..., None]
    return vals.transpose(0, 1, 3, 2).reshape(g * 512, n)
def pack4(w):
    words, scales = pack_weight(w, "e2m1")
    return words.reshape(words.shape[0], 128, -1), scales


def unpack4(words, scales):
    return unpack_weight(words.reshape(words.shape[0], 128, -1, 2), scales, "e2m1")


M, K, N, R, V = 1024, 1024, 2048, 512, 512


def setup_inputs():
    s, t, u = mx_kscale(K), mx_kscale(N), mx_kscale(M)
    busy = np.random.uniform(0.3, 1.0, (M, 1))
    load = np.random.uniform(0.3, 0.65, N)
    arrivals = np.random.standard_exponential((M, K)) * busy
    visits = np.random.standard_exponential((K, N)) * load / K
    holding = np.random.uniform(0.5, 3.5, (M, N))
    c = np.random.standard_normal((N, R)) / np.sqrt(N)
    c_words, c_scales = pack4(c / t[:, None])
    return {"arrivals": bf(arrivals * s),
            "visits": bf(visits / s[:, None]),
            "holding": bf(holding * t * u[:, None]),
            "c_words": c_words,
            "c_scales": c_scales,
            "contrasts": bf(np.random.standard_normal((V, M)) / np.sqrt(M) / u)}


def reference(arrivals, visits, holding, c_words, c_scales, contrasts):
    rho = mxq(f64(arrivals), 1, "e4m3") @ mxq(f64(visits), 0, "e4m3")
    cost = rho / (1.0 - rho) * f64(holding)
    account = mxq(cost, 1, "e4m3") @ unpack4(c_words, c_scales)
    contrast = mxq(f64(contrasts), 1, "e4m3") @ mxq(cost, 0, "e4m3")
    return account, contrast

@@ -1,0 +1,444 @@
+from contextlib import ExitStack
+
+import concourse.mybir as mybir
+from concourse.masks import make_identity
+
+M, K, N, R, V = 1024, 1024, 2048, 512, 512
+FLOPS = 2 * M * K * N + 2 * M * N * R + 2 * V * M * N
+
+F32 = mybir.dt.float32
+BF16 = mybir.dt.bfloat16
+I32 = mybir.dt.int32
+U32 = mybir.dt.uint32
+U8 = mybir.dt.uint8
+FP8X4 = mybir.dt.float8_e4m3fn_x4
+FP4X4 = mybir.dt.float4_e2m1fn_x4
+ACT = mybir.ActivationFunctionType
+MULT = mybir.AluOpType.mult
+
+P = 128
+PACK = 4
+W = 512
+ORDER = [(0, 0), (1, 0), (0, 1), (0, 2), (0, 3), (1, 1), (1, 2), (1, 3)]
+HEAD_SPLIT = 336
+VISITS_PACK_VECTOR = {0: (1, 0), 1: (1, 1), 3: (2, 1)}
+VISITS_PACK_SCALAR = {2: (2, 0), 4: (3, 0), 6: (3, 1)}
+VISITS_QUANTIZE = {1: (1, 0), 2: (1, 1), 3: (2, 0), 4: (2, 1), 5: (3, 0)}
+ROWS_TURN = {0: (4, 5), 1: (6, 7), 3: (8, 9), 5: (10, 11)}
+ROWS_QUANTIZE = {0: (4, 5), 1: (6, 7), 5: (8, 9, 10, 11)}
+COST_N_QUANTIZE = {4: 0, 6: 1, 8: 2, 10: 3, 11: 4, 14: 5, 15: 6}
+OUTPUTS = {
+    8: [("contrast", 0, 0, "scalar"), ("contrast", 0, 1, "scalar")],
+    10: [("contrast", 0, 2, "scalar"), ("contrast", 0, 3, "scalar")],
+    12: [("account", 0, 0, "scalar"), ("account", 0, 1, "scalar")],
+    13: [("account", 0, 2, "vector"), ("account", 0, 3, "vector")],
+    14: [("contrast", 1, 0, "scalar"), ("contrast", 1, 1, "scalar"), ("contrast", 1, 2, "scalar"), ("contrast", 1, 3, "scalar")],
+    15: [("contrast", 2, 0, "scalar"), ("contrast", 2, 1, "vector")],
+}
+
+
+def tile_jackson_congestion_cost_s8_kernel(
+    tc, arrivals, visits, holding, c_words, c_scales, contrasts, out_0, out_1
+):
+    nc = tc.nc
+    with ExitStack() as ctx:
+        sb = ctx.enter_context(tc.tile_pool(name="sb", bufs=1))
+        ps = ctx.enter_context(tc.psum_pool(name="ps", bufs=1))
+
+        def tiles(name, count, shape, dtype):
+            return [sb.tile(shape, dtype, name="%s%d" % (name, i), align_bytes=64) for i in range(count)]
+
+        banks = [ps.tile([P, W], F32, name="bank%d" % i) for i in range(8)]
+        rho_banks, turn_banks, out_banks = banks[0:4], banks[4:6], banks[6:8]
+
+        ident = sb.tile([P, P], F32, name="ident")
+        warm = sb.tile([P, 2], F32, name="warm")
+        rows_raw = tiles("rows_raw", 2, [P, PACK, K], BF16)
+        vis_raw = tiles("vis_raw", 4, [P, PACK, W], BF16)
+        hold = tiles("hold", 8, [P, PACK, W], BF16)
+        c_codes = sb.tile([P, 4, 2 * R], U8, name="c_codes", align_bytes=64)
+        c_plane = sb.tile([P, 4, R], U8, name="c_plane", align_bytes=64)
+
+        vis_packed = tiles("vis_packed", 3, [P, W, PACK], BF16)
+        vis_codes = tiles("vis_codes", 8, [P, W], U32)
+        vis_scales = tiles("vis_scales", 8, [P, W], U8)
+        rows_packed = tiles("rows_packed", 4, [P, 2, P, PACK], BF16)
+        rows_codes = tiles("rows_codes", 12, [P, 2, P], U32)
+        rows_scales = tiles("rows_scales", 12, [P, 2, P], U8)
+        idle_sq = tiles("idle_sq", 1, [P, 2, W], F32)
+        inv_idle = tiles("inv_idle", 3, [P, 2, W], F32)
+        weighted = tiles("weighted", 2, [P, 2, W], F32)
+        cost = tiles("cost", 2, [P, PACK, W], BF16)
+        cost_m_packed = tiles("cost_m_packed", 2, [P, W, PACK], BF16)
+        cost_m_codes = tiles("cost_m_codes", 8, [P, W], U32)
+        cost_m_scales = tiles("cost_m_scales", 8, [P, W], U8)
+        cost_n_packed = tiles("cost_n_packed", 2, [P, PACK, P, PACK], BF16)
+        cost_n_codes = tiles("cost_n_codes", 8, [P, W], U32)
+        cost_n_scales = tiles("cost_n_scales", 8, [P, W], U8)
+        result = tiles("result", 8, [P, W], F32)
+
+        def copy_on(engine, out, in_):
+            if engine == "scalar":
+                nc.scalar.copy(out=out, in_=in_)
+            else:
+                nc.vector.tensor_copy(out=out, in_=in_)
+
+        def interleave(engine, packed, rows, n0, n1):
+            copy_on(
+                engine,
+                packed[:, n0:n1, :].rearrange("p (c i) t -> p c t i", i=4),
+                rows[:, :, n0:n1].rearrange("p t (c i) -> p c t i", i=4),
+            )
+
+        def quantize(codes, scales, packed):
+            nc.vector.quantize_mx(out=codes.bitcast(FP8X4), scales=scales, in_=packed)
+
+        def turn(bank, slot, words):
+            halves = bank[:].rearrange("p (s u r) -> p s u r", s=2, u=2)
+            for u in range(2):
+                nc.tensor.transpose(halves[:, slot, u, :], words[:, u : 256 : 2], ident[:])
+
+        def unturn(engine, packed, bank):
+            copy_on(
+                engine,
+                packed.rearrange("p s r t -> p s (r t)").bitcast(F32).rearrange("p s (r u) -> p s r u", u=2),
+                bank[:].rearrange("p (s u r) -> p s r u", s=2, u=2),
+            )
+
+        def load_rows(i, t0, t1):
+            src = arrivals[i * W : (i + 1) * W, :] if i < 2 else contrasts
+            nc.sync.dma_start(
+                out=rows_raw[i % 2][:, t0:t1, :], in_=src.rearrange("(p t) k -> p t k", t=PACK)[:, t0:t1, :]
+            )
+
+        def load_visits(j, kp):
+            nc.sync.dma_start(
+                out=vis_raw[(2 * j + kp) % 4][:],
+                in_=visits[kp * W : (kp + 1) * W, j * W : (j + 1) * W].rearrange("(p t) n -> p t n", t=PACK),
+            )
+
+        def load_hold(s, t0, t1):
+            g, j = ORDER[s]
+            nc.sync.dma_start(
+                out=hold[s][:, t0:t1, :],
+                in_=holding[g * W : (g + 1) * W, j * W : (j + 1) * W].rearrange("(p t) n -> p t n", t=PACK)[:, t0:t1, :],
+            )
+
+        def load_c():
+            for q in range(4):
+                nc.sync.dma_start(
+                    out=c_plane[32 * q : 32 * q + 4, :, :].bitcast(I32),
+                    in_=c_scales[:, 4 * q : 4 * q + 4, :].rearrange("g r n -> r g n").bitcast(I32),
+                )
+            nc.sync.dma_start(out=c_codes[:].bitcast(I32), in_=c_words.rearrange("g p b -> p g b").bitcast(I32))
+
+        def visits_pack(engine, j, kp, n0, n1):
+            i = 2 * j + kp
+            interleave(engine, vis_packed[i % 3], vis_raw[i % 4], n0, n1)
+
+        def visits_quantize(j, kp):
+            i = 2 * j + kp
+            quantize(vis_codes[i][:], vis_scales[i][:], vis_packed[i % 3][:].rearrange("p n t -> p (n t)"))
+
+        def rows_turn(i):
+            words = rows_raw[(i // 4) % 2][:, i % 4, :].bitcast(F32)
+            for kp in range(2):
+                turn(turn_banks[i % 2], kp, words[:, 256 * kp : 256 * (kp + 1)])
+
+        def rows_unturn(engine, i):
+            unturn(engine, rows_packed[i % 4][:], turn_banks[i % 2])
+
+        def rows_quantize(i):
+            quantize(
+                rows_codes[i][:].rearrange("p s r -> p (s r)"),
+                rows_scales[i][:].rearrange("p s r -> p (s r)"),
+                rows_packed[i % 4][:].rearrange("p s r t -> p (s r t)"),
+            )
+
+        def pieces(k):
+            s, e = k // 4, k % 4
+            if k < 30:
+                return [(e, 0, W, 0)]
+            return [(t, (k - 30) * 256, 256, (t - 2) * 256) for t in (2, 3)]
+
+        def region(tile, k):
+            if k < 30:
+                return tile[:, k % 4, :]
+            return tile[:, 2:4, (k - 30) * 256 : (k - 29) * 256]
+
+        def like(flat, k):
+            return flat if k < 30 else flat.rearrange("p (t n) -> p t n", t=2)
+
+        def rho_matmul(k):
+            g, j = ORDER[k // 4]
+            for t, n0, width, col in pieces(k):
+                for kp in range(2):
+                    nc.tensor.matmul_mx(
+                        out=rho_banks[k % 4][:, col : col + width],
+                        lhsT=rows_codes[4 * g + t][:, kp, :].bitcast(FP8X4),
+                        lhsT_scale=rows_scales[4 * g + t][:, kp, :],
+                        rhs=vis_codes[2 * j + kp][:, n0 : n0 + width].bitcast(FP8X4),
+                        rhs_scale=vis_scales[2 * j + kp][:, n0 : n0 + width],
+                        start=(kp == 0),
+                        stop=(kp == 1),
+                    )
+
+        def square_idle(k):
+            nc.scalar.activation(
+                out=idle_sq[0][:, k % 2, :], in_=rho_banks[k % 4][:], func=ACT.Square, bias=1.0, scale=-1.0
+            )
+
+        def invert_idle(k):
+            nc.scalar.activation(
+                out=inv_idle[(k // 2) % 3][:, k % 2, :], in_=idle_sq[0][:, k % 2, :], func=ACT.Abs_reciprocal_sqrt
+            )
+
+        def weigh(k):
+            nc.vector.tensor_tensor(
+                out=like(weighted[(k // 2) % 2][:, k % 2, :], k),
+                in0=like(rho_banks[k % 4][:], k),
+                in1=region(hold[k // 4], k),
+                op=MULT,
+            )
+
+        def finish_pair(c):
+            t0 = 2 * (c % 2)
+            nc.vector.tensor_tensor(
+                out=cost[(c // 2) % 2][:, t0 : t0 + 2, :], in0=weighted[c % 2][:], in1=inv_idle[c % 3][:], op=MULT
+            )
+
+        def finish_bank(k):
+            nc.vector.tensor_tensor(
+                out=region(cost[(k // 4) % 2], k),
+                in0=like(weighted[(k // 2) % 2][:, k % 2, :], k),
+                in1=like(inv_idle[(k // 2) % 3][:, k % 2, :], k),
+                op=MULT,
+            )
+
+        def cost_pack(engine, s, n0, n1):
+            interleave(engine, cost_m_packed[s % 2], cost[s % 2], n0, n1)
+
+        def cost_m_quantize(s, n0, n1):
+            quantize(
+                cost_m_codes[s][:, n0:n1],
+                cost_m_scales[s][:, n0:n1],
+                cost_m_packed[s % 2][:, n0:n1, :].rearrange("p n t -> p (n t)"),
+            )
+
+        def cost_turn(s, h):
+            for slot in range(2):
+                turn(turn_banks[h], slot, cost[s % 2][:, 2 * h + slot, :].bitcast(F32))
+
+        def cost_unturn(engine, s, h):
+            unturn(engine, cost_n_packed[s % 2][:, 2 * h : 2 * h + 2, :, :], turn_banks[h])
+
+        def cost_n_quantize(s, h0, h1):
+            cols = slice(256 * h0, 256 * h1)
+            quantize(
+                cost_n_codes[s][:, cols],
+                cost_n_scales[s][:, cols],
+                cost_n_packed[s % 2][:, 2 * h0 : 2 * h1, :, :].rearrange("p s r t -> p (s r t)"),
+            )
+
+        def account_matmul(bank, g, t, j0, j1):
+            cols = slice(P * t, P * (t + 1))
+            for j in range(j0, j1):
+                s = ORDER.index((g, j))
+                nc.tensor.matmul_mx(
+                    out=bank[:],
+                    lhsT=cost_n_codes[s][:, cols].bitcast(FP8X4),
+                    lhsT_scale=cost_n_scales[s][:, cols],
+                    rhs=c_codes[:, j, :].bitcast(FP4X4),
+                    rhs_scale=c_plane[:, j, :],
+                    start=(j == 0),
+                    stop=(j == 3),
+                )
+
+        def contrast_matmul(out, j, t, n0, n1):
+            for g in range(2):
+                s = ORDER.index((g, j))
+                nc.tensor.matmul_mx(
+                    out=out,
+                    lhsT=rows_codes[8 + t][:, g, :].bitcast(FP8X4),
+                    lhsT_scale=rows_scales[8 + t][:, g, :],
+                    rhs=cost_m_codes[s][:, n0:n1].bitcast(FP8X4),
+                    rhs_scale=cost_m_scales[s][:, n0:n1],
+                    start=(g == 0),
+                    stop=(g == 1),
+                )
+
+        account_rows = out_0.rearrange("(g p t) r -> g t p r", g=2, t=PACK)
+        contrast_rows = out_1.rearrange("(p t) n -> t p n", t=PACK)
+
+        stored = []
+
+        def store(engine, bank, dst):
+            n = len(stored)
+            stored.append(dst)
+            copy_on(engine, result[n % 8][:], bank[:])
+            nc.sync.dma_start(out=dst, in_=result[n % 8][:])
+
+        def contrast_out(engine, j, t, bank):
+            store(engine, bank, contrast_rows[t, :, j * W : (j + 1) * W])
+
+        def account_out(engine, g, t, bank):
+            store(engine, bank, account_rows[g, t])
+
+        def contrast_half(half, pair):
+            for t in range(4):
+                contrast_matmul(pair[t // 2][:, (t % 2) * 256 : (t % 2 + 1) * 256], 3, t, 256 * half, 256 * (half + 1))
+
+        def contrast_half_out(engine, half, h, bank):
+            n0 = 3 * W + 256 * half
+            n = len(stored)
+            stored.append(half)
+            copy_on(engine, result[n % 8][:], bank[:])
+            nc.sync.dma_start(
+                out=out_1.rearrange("(p t) n -> p t n", t=PACK)[:, 2 * h : 2 * h + 2, n0 : n0 + 256],
+                in_=result[n % 8][:].rearrange("p (t n) -> p t n", t=2),
+            )
+
+        def early_vector(c):
+            if c % 2 == 1 and c >= 3:
+                cost_m_quantize((c - 3) // 2, 0, W)
+            if c == 7:
+                visits_quantize(3, 1)
+
+        def late_vector(c):
+            if c in VISITS_QUANTIZE:
+                visits_quantize(*VISITS_QUANTIZE[c])
+            if c in COST_N_QUANTIZE:
+                cost_n_quantize(COST_N_QUANTIZE[c], 0, 2)
+            if c % 2 == 0 and c >= 2:
+                cost_pack("vector", (c - 2) // 2, 0, W)
+            if c in VISITS_PACK_VECTOR:
+                visits_pack("vector", *VISITS_PACK_VECTOR[c], 0, W)
+            for i in ROWS_QUANTIZE.get(c, ()):
+                rows_quantize(i)
+
+        def feed_scalar(c):
+            if c % 2 == 1 and c >= 3:
+                s = (c - 3) // 2
+                for h in range(2):
+                    cost_turn(s, h)
+                for h in range(2):
+                    cost_unturn("scalar", s, h)
+            for i in ROWS_TURN.get(c, ()):
+                rows_turn(i)
+            for i in ROWS_TURN.get(c, ()):
+                rows_unturn("scalar", i)
+            if c in VISITS_PACK_SCALAR:
+                visits_pack("scalar", *VISITS_PACK_SCALAR[c], 0, W)
+            for kind, i, t, engine in OUTPUTS.get(c, ()):
+                if kind == "contrast":
+                    contrast_matmul(out_banks[t % 2][:], i, t, 0, W)
+                else:
+                    account_matmul(out_banks[t % 2], i, t, 0, 4)
+                if engine == "scalar":
+                    (contrast_out if kind == "contrast" else account_out)(engine, i, t, out_banks[t % 2])
+
+        def vector_outputs(c):
+            for kind, i, t, engine in OUTPUTS.get(c, ()):
+                if engine == "vector":
+                    (contrast_out if kind == "contrast" else account_out)(engine, i, t, out_banks[t % 2])
+
+        with tc.manual_schedule(engines={mybir.EngineType.SP}):
+            load_visits(0, 0)
+            load_rows(0, 0, 1)
+            load_visits(0, 1)
+            load_rows(0, 1, 2)
+            load_rows(0, 2, 4)
+            load_hold(0, 0, 2)
+            load_visits(1, 0)
+            load_rows(1, 0, 2)
+            load_hold(0, 2, 4)
+            load_rows(1, 2, 4)
+            load_visits(1, 1)
+            load_hold(1, 0, 4)
+            make_identity(nc, ident[:])
+            nc.vector.memset(warm[:, 0:1], 1.0)
+            nc.scalar.activation(out=warm[:, 1:2], in_=warm[:, 0:1], func=ACT.Abs_reciprocal_sqrt)
+            nc.vector.memset(c_plane[:].rearrange("p g n -> p (g n)").bitcast(I32), 0)
+
+            visits_pack("vector", 0, 0, 0, HEAD_SPLIT)
+            visits_pack("scalar", 0, 0, HEAD_SPLIT, W)
+            rows_turn(0)
+            rows_unturn("scalar", 0)
+            visits_quantize(0, 0)
+            rows_turn(1)
+            visits_pack("vector", 0, 1, 0, W)
+            rows_unturn("scalar", 1)
+            rows_quantize(0)
+            visits_quantize(0, 1)
+            rows_quantize(1)
+            load_visits(2, 0)
+            load_visits(2, 1)
+            rho_matmul(0)
+            rho_matmul(1)
+            rows_turn(2)
+            rows_turn(3)
+            load_rows(2, 0, 4)
+            load_hold(2, 0, 4)
+            rows_unturn("scalar", 2)
+            rows_unturn("scalar", 3)
+            rows_quantize(2)
+            rows_quantize(3)
+
+            for c in range(16):
+                for k in (2 * c, 2 * c + 1):
+                    square_idle(k)
+                for k in (2 * c, 2 * c + 1):
+                    invert_idle(k)
+                weigh(2 * c)
+                early_vector(c)
+                weigh(2 * c + 1)
+                if c < 15:
+                    rho_matmul(2 * c + 2)
+                    rho_matmul(2 * c + 3)
+                feed_scalar(c)
+                if c > 0:
+                    finish_pair(c - 1)
+                late_vector(c)
+                vector_outputs(c)
+                if c == 0:
+                    load_visits(3, 0)
+                    load_hold(3, 0, 4)
+                    load_hold(4, 0, 4)
+                if c == 1:
+                    load_visits(3, 1)
+                    for s in range(5, 8):
+                        load_hold(s, 0, 4)
+                    load_c()
+
+            for t in range(2, 4):
+                contrast_matmul(out_banks[t % 2][:], 2, t, 0, W)
+            cost_turn(7, 0)
+            finish_bank(30)
+            cost_unturn("scalar", 7, 0)
+            contrast_out("scalar", 2, 2, out_banks[0])
+            contrast_out("scalar", 2, 3, out_banks[1])
+            finish_bank(31)
+            cost_turn(7, 1)
+            for t in range(4):
+                account_matmul(rho_banks[t], 1, t, 0, 3)
+            cost_pack("vector", 7, 0, 256)
+            cost_n_quantize(7, 0, 1)
+            cost_m_quantize(7, 0, 256)
+            cost_unturn("scalar", 7, 1)
+            for t in range(2):
+                account_matmul(rho_banks[t], 1, t, 3, 4)
+            cost_pack("vector", 7, 256, W)
+            contrast_half(0, out_banks)
+            for t in range(2):
+                account_out("scalar", 1, t, rho_banks[t])
+            cost_n_quantize(7, 1, 2)
+            cost_m_quantize(7, 256, W)
+            for t in range(2, 4):
+                account_matmul(rho_banks[t], 1, t, 3, 4)
+            contrast_half(1, turn_banks)
+            contrast_half_out("vector", 0, 0, out_banks[0])
+            contrast_half_out("scalar", 0, 1, out_banks[1])
+            account_out("vector", 1, 2, rho_banks[2])
+            account_out("scalar", 1, 3, rho_banks[3])
+            contrast_half_out("vector", 1, 0, turn_banks[0])
+            contrast_half_out("scalar", 1, 1, turn_banks[1])

@@ -21,19 +21,27 @@ PACK = 4
 W = 512
 ORDER = [(0, 0), (1, 0), (0, 1), (0, 2), (0, 3), (1, 1), (1, 2), (1, 3)]
 HEAD_SPLIT = 336
-VISITS_PACK_VECTOR = {0: (1, 0), 1: (1, 1), 3: (2, 1)}
-VISITS_PACK_SCALAR = {2: (2, 0), 4: (3, 0), 6: (3, 1)}
-VISITS_QUANTIZE = {1: (1, 0), 2: (1, 1), 3: (2, 0), 4: (2, 1), 5: (3, 0)}
-ROWS_TURN = {0: (4, 5), 1: (6, 7), 3: (8, 9), 5: (10, 11)}
-ROWS_QUANTIZE = {0: (4, 5), 1: (6, 7), 5: (8, 9, 10, 11)}
-COST_N_QUANTIZE = {4: 0, 6: 1, 8: 2, 10: 3, 11: 4, 14: 5, 15: 6}
+VISITS_PACK = {
+    1: [("vector", 2, 0, 0, 512)],
+    3: [("vector", 2, 1, 0, 512)],
+    4: [("scalar", 3, 0, 0, 512)],
+    5: [("vector", 3, 1, 0, 512)],
+}
+COST_PACK = {6: "scalar"}
+VISITS_QUANTIZE = {4: 2, 6: 3}
+ROWS_UNTURN = {0: (4, 5), 1: (6, 7), 3: (8, 9), 5: (10, 11)}
+ROWS_QUANTIZE = {1: 4, 2: 6, 5: 8, 7: 10}
+COST_QUANTIZE_BEFORE = {
+    3: [(0, 0, 1024)], 5: [(1, 0, 1024)], 8: [(2, 0, 1024)], 9: [(3, 0, 1024)], 10: [(4, 512, 768)],
+    11: [(4, 768, 1024), (4, 0, 512)], 13: [(5, 512, 1024)],
+}
+COST_QUANTIZE_AFTER = {12: [(5, 0, 512)], 14: [(6, 0, 512)]}
 OUTPUTS = {
     8: [("contrast", 0, 0, "scalar"), ("contrast", 0, 1, "scalar")],
-    10: [("contrast", 0, 2, "scalar"), ("contrast", 0, 3, "scalar")],
-    12: [("account", 0, 0, "scalar"), ("account", 0, 1, "scalar")],
-    13: [("account", 0, 2, "vector"), ("account", 0, 3, "vector")],
-    14: [("contrast", 1, 0, "scalar"), ("contrast", 1, 1, "scalar"), ("contrast", 1, 2, "scalar"), ("contrast", 1, 3, "scalar")],
-    15: [("contrast", 2, 0, "scalar"), ("contrast", 2, 1, "vector")],
+    9: [("contrast", 0, 2, "scalar"), ("contrast", 0, 3, "scalar")],
+    10: [("account", 0, 0, "scalar"), ("account", 0, 1, "scalar")],
+    11: [("account", 0, 2, "scalar"), ("account", 0, 3, "scalar")],
+    12: [("contrast", 1, 0, "scalar"), ("contrast", 1, 1, "scalar")],
 }
 
 
@@ -55,27 +63,24 @@ def tile_jackson_congestion_cost_s8_kernel(
         warm = sb.tile([P, 2], F32, name="warm")
         rows_raw = tiles("rows_raw", 2, [P, PACK, K], BF16)
         vis_raw = tiles("vis_raw", 4, [P, PACK, W], BF16)
-        hold = tiles("hold", 8, [P, PACK, W], BF16)
+        hold = tiles("hold", 7, [P, PACK, W], BF16)
         c_codes = sb.tile([P, 4, 2 * R], U8, name="c_codes", align_bytes=64)
         c_plane = sb.tile([P, 4, R], U8, name="c_plane", align_bytes=64)
 
-        vis_packed = tiles("vis_packed", 3, [P, W, PACK], BF16)
-        vis_codes = tiles("vis_codes", 8, [P, W], U32)
-        vis_scales = tiles("vis_scales", 8, [P, W], U8)
-        rows_packed = tiles("rows_packed", 4, [P, 2, P, PACK], BF16)
-        rows_codes = tiles("rows_codes", 12, [P, 2, P], U32)
-        rows_scales = tiles("rows_scales", 12, [P, 2, P], U8)
-        idle_sq = tiles("idle_sq", 1, [P, 2, W], F32)
+        vis_packed = tiles("vis_packed", 2, [P, 2, W, PACK], BF16)
+        vis_codes = tiles("vis_codes", 4, [P, 2, W], U32)
+        vis_scales = tiles("vis_scales", 4, [P, 2, W], U8)
+        rows_packed = tiles("rows_packed", 2, [P, 2, 2, P, PACK], BF16)
+        rows_codes = tiles("rows_codes", 6, [P, 2, 2, P], U32)
+        rows_scales = tiles("rows_scales", 6, [P, 2, 2, P], U8)
+        idle_sq = tiles("idle_sq", 2, [P, 2, W], F32)
         inv_idle = tiles("inv_idle", 3, [P, 2, W], F32)
         weighted = tiles("weighted", 2, [P, 2, W], F32)
         cost = tiles("cost", 2, [P, PACK, W], BF16)
-        cost_m_packed = tiles("cost_m_packed", 2, [P, W, PACK], BF16)
-        cost_m_codes = tiles("cost_m_codes", 8, [P, W], U32)
-        cost_m_scales = tiles("cost_m_scales", 8, [P, W], U8)
-        cost_n_packed = tiles("cost_n_packed", 2, [P, PACK, P, PACK], BF16)
-        cost_n_codes = tiles("cost_n_codes", 8, [P, W], U32)
-        cost_n_scales = tiles("cost_n_scales", 8, [P, W], U8)
-        result = tiles("result", 8, [P, W], F32)
+        cost_packed = tiles("cost_packed", 2, [P, 2, W, PACK], BF16)
+        cost_codes = tiles("cost_codes", 8, [P, 2, W], U32)
+        cost_scales = tiles("cost_scales", 8, [P, 2, W], U8)
+        result = tiles("result", 7, [P, W], F32)
 
         def copy_on(engine, out, in_):
             if engine == "scalar":
@@ -120,7 +125,7 @@ def tile_jackson_congestion_cost_s8_kernel(
         def load_hold(s, t0, t1):
             g, j = ORDER[s]
             nc.sync.dma_start(
-                out=hold[s][:, t0:t1, :],
+                out=hold[s % 7][:, t0:t1, :],
                 in_=holding[g * W : (g + 1) * W, j * W : (j + 1) * W].rearrange("(p t) n -> p t n", t=PACK)[:, t0:t1, :],
             )
 
@@ -134,25 +139,29 @@ def tile_jackson_congestion_cost_s8_kernel(
 
         def visits_pack(engine, j, kp, n0, n1):
             i = 2 * j + kp
-            interleave(engine, vis_packed[i % 3], vis_raw[i % 4], n0, n1)
+            interleave(engine, vis_packed[j % 2][:, kp, :, :], vis_raw[i % 4], n0, n1)
 
-        def visits_quantize(j, kp):
-            i = 2 * j + kp
-            quantize(vis_codes[i][:], vis_scales[i][:], vis_packed[i % 3][:].rearrange("p n t -> p (n t)"))
+        def visits_quantize(j, kp0, kp1):
+            quantize(
+                vis_codes[j][:, kp0:kp1, :].rearrange("p s n -> p (s n)"),
+                vis_scales[j][:, kp0:kp1, :].rearrange("p s n -> p (s n)"),
+                vis_packed[j % 2][:, kp0:kp1, :, :].rearrange("p s n t -> p (s n t)"),
+            )
 
-        def rows_turn(i):
+        def rows_turn(i, bank):
             words = rows_raw[(i // 4) % 2][:, i % 4, :].bitcast(F32)
             for kp in range(2):
-                turn(turn_banks[i % 2], kp, words[:, 256 * kp : 256 * (kp + 1)])
+                turn(bank, kp, words[:, 256 * kp : 256 * (kp + 1)])
 
-        def rows_unturn(engine, i):
-            unturn(engine, rows_packed[i % 4][:], turn_banks[i % 2])
+        def rows_unturn(engine, i, bank):
+            unturn(engine, rows_packed[(i // 2) % 2][:, i % 2, :, :, :], bank)
 
-        def rows_quantize(i):
+        def rows_quantize(i, count):
+            e = slice(i % 2, i % 2 + count)
             quantize(
-                rows_codes[i][:].rearrange("p s r -> p (s r)"),
-                rows_scales[i][:].rearrange("p s r -> p (s r)"),
-                rows_packed[i % 4][:].rearrange("p s r t -> p (s r t)"),
+                rows_codes[i // 2][:, e, :, :].rearrange("p e s r -> p (e s r)"),
+                rows_scales[i // 2][:, e, :, :].rearrange("p e s r -> p (e s r)"),
+                rows_packed[(i // 2) % 2][:, e, :, :, :].rearrange("p e s r t -> p (e s r t)"),
             )
 
         def pieces(k):
@@ -175,29 +184,29 @@ def tile_jackson_congestion_cost_s8_kernel(
                 for kp in range(2):
                     nc.tensor.matmul_mx(
                         out=rho_banks[k % 4][:, col : col + width],
-                        lhsT=rows_codes[4 * g + t][:, kp, :].bitcast(FP8X4),
-                        lhsT_scale=rows_scales[4 * g + t][:, kp, :],
-                        rhs=vis_codes[2 * j + kp][:, n0 : n0 + width].bitcast(FP8X4),
-                        rhs_scale=vis_scales[2 * j + kp][:, n0 : n0 + width],
+                        lhsT=rows_codes[2 * g + t // 2][:, t % 2, kp, :].bitcast(FP8X4),
+                        lhsT_scale=rows_scales[2 * g + t // 2][:, t % 2, kp, :],
+                        rhs=vis_codes[j][:, kp, n0 : n0 + width].bitcast(FP8X4),
+                        rhs_scale=vis_scales[j][:, kp, n0 : n0 + width],
                         start=(kp == 0),
                         stop=(kp == 1),
                     )
 
         def square_idle(k):
             nc.scalar.activation(
-                out=idle_sq[0][:, k % 2, :], in_=rho_banks[k % 4][:], func=ACT.Square, bias=1.0, scale=-1.0
+                out=idle_sq[(k // 2) % 2][:, k % 2, :], in_=rho_banks[k % 4][:], func=ACT.Square, bias=1.0, scale=-1.0
             )
 
-        def invert_idle(k):
+        def invert_idle(c, e0, e1):
             nc.scalar.activation(
-                out=inv_idle[(k // 2) % 3][:, k % 2, :], in_=idle_sq[0][:, k % 2, :], func=ACT.Abs_reciprocal_sqrt
+                out=inv_idle[c % 3][:, e0:e1, :], in_=idle_sq[c % 2][:, e0:e1, :], func=ACT.Abs_reciprocal_sqrt
             )
 
         def weigh(k):
             nc.vector.tensor_tensor(
                 out=like(weighted[(k // 2) % 2][:, k % 2, :], k),
                 in0=like(rho_banks[k % 4][:], k),
-                in1=region(hold[k // 4], k),
+                in1=region(hold[(k // 4) % 7], k),
                 op=MULT,
             )
 
@@ -216,28 +225,21 @@ def tile_jackson_congestion_cost_s8_kernel(
             )
 
         def cost_pack(engine, s, n0, n1):
-            interleave(engine, cost_m_packed[s % 2], cost[s % 2], n0, n1)
+            interleave(engine, cost_packed[s % 2][:, 0, :, :], cost[s % 2], n0, n1)
 
-        def cost_m_quantize(s, n0, n1):
-            quantize(
-                cost_m_codes[s][:, n0:n1],
-                cost_m_scales[s][:, n0:n1],
-                cost_m_packed[s % 2][:, n0:n1, :].rearrange("p n t -> p (n t)"),
-            )
-
-        def cost_turn(s, h):
+        def cost_turn(s, h, bank):
             for slot in range(2):
-                turn(turn_banks[h], slot, cost[s % 2][:, 2 * h + slot, :].bitcast(F32))
+                turn(bank, slot, cost[s % 2][:, 2 * h + slot, :].bitcast(F32))
 
-        def cost_unturn(engine, s, h):
-            unturn(engine, cost_n_packed[s % 2][:, 2 * h : 2 * h + 2, :, :], turn_banks[h])
+        def cost_unturn(engine, s, h, bank):
+            packed = cost_packed[s % 2][:, 1, 256 * h : 256 * (h + 1), :]
+            unturn(engine, packed.rearrange("p (s r) t -> p s r t", s=2), bank)
 
-        def cost_n_quantize(s, h0, h1):
-            cols = slice(256 * h0, 256 * h1)
+        def cost_quantize(s, c0, c1):
             quantize(
-                cost_n_codes[s][:, cols],
-                cost_n_scales[s][:, cols],
-                cost_n_packed[s % 2][:, 2 * h0 : 2 * h1, :, :].rearrange("p s r t -> p (s r t)"),
+                cost_codes[s][:].rearrange("p a n -> p (a n)")[:, c0:c1],
+                cost_scales[s][:].rearrange("p a n -> p (a n)")[:, c0:c1],
+                cost_packed[s % 2][:].rearrange("p a n t -> p (a n t)")[:, PACK * c0 : PACK * c1],
             )
 
         def account_matmul(bank, g, t, j0, j1):
@@ -246,8 +248,8 @@ def tile_jackson_congestion_cost_s8_kernel(
                 s = ORDER.index((g, j))
                 nc.tensor.matmul_mx(
                     out=bank[:],
-                    lhsT=cost_n_codes[s][:, cols].bitcast(FP8X4),
-                    lhsT_scale=cost_n_scales[s][:, cols],
+                    lhsT=cost_codes[s][:, 1, cols].bitcast(FP8X4),
+                    lhsT_scale=cost_scales[s][:, 1, cols],
                     rhs=c_codes[:, j, :].bitcast(FP4X4),
                     rhs_scale=c_plane[:, j, :],
                     start=(j == 0),
@@ -259,10 +261,10 @@ def tile_jackson_congestion_cost_s8_kernel(
                 s = ORDER.index((g, j))
                 nc.tensor.matmul_mx(
                     out=out,
-                    lhsT=rows_codes[8 + t][:, g, :].bitcast(FP8X4),
-                    lhsT_scale=rows_scales[8 + t][:, g, :],
-                    rhs=cost_m_codes[s][:, n0:n1].bitcast(FP8X4),
-                    rhs_scale=cost_m_scales[s][:, n0:n1],
+                    lhsT=rows_codes[4 + t // 2][:, t % 2, g, :].bitcast(FP8X4),
+                    lhsT_scale=rows_scales[4 + t // 2][:, t % 2, g, :],
+                    rhs=cost_codes[s][:, 0, n0:n1].bitcast(FP8X4),
+                    rhs_scale=cost_scales[s][:, 0, n0:n1],
                     start=(g == 0),
                     stop=(g == 1),
                 )
@@ -275,8 +277,8 @@ def tile_jackson_congestion_cost_s8_kernel(
         def store(engine, bank, dst):
             n = len(stored)
             stored.append(dst)
-            copy_on(engine, result[n % 8][:], bank[:])
-            nc.sync.dma_start(out=dst, in_=result[n % 8][:])
+            copy_on(engine, result[n % 7][:], bank[:])
+            nc.sync.dma_start(out=dst, in_=result[n % 7][:])
 
         def contrast_out(engine, j, t, bank):
             store(engine, bank, contrast_rows[t, :, j * W : (j + 1) * W])
@@ -292,69 +294,36 @@ def tile_jackson_congestion_cost_s8_kernel(
             n0 = 3 * W + 256 * half
             n = len(stored)
             stored.append(half)
-            copy_on(engine, result[n % 8][:], bank[:])
+            copy_on(engine, result[n % 7][:], bank[:])
             nc.sync.dma_start(
                 out=out_1.rearrange("(p t) n -> p t n", t=PACK)[:, 2 * h : 2 * h + 2, n0 : n0 + 256],
-                in_=result[n % 8][:].rearrange("p (t n) -> p t n", t=2),
+                in_=result[n % 7][:].rearrange("p (t n) -> p t n", t=2),
             )
 
-        def early_vector(c):
-            if c % 2 == 1 and c >= 3:
-                cost_m_quantize((c - 3) // 2, 0, W)
-            if c == 7:
-                visits_quantize(3, 1)
+        def output_matmul(kind, i, t):
+            if kind == "contrast":
+                contrast_matmul(out_banks[t % 2][:], i, t, 0, W)
+            else:
+                account_matmul(out_banks[t % 2], i, t, 0, 4)
 
-        def late_vector(c):
-            if c in VISITS_QUANTIZE:
-                visits_quantize(*VISITS_QUANTIZE[c])
-            if c in COST_N_QUANTIZE:
-                cost_n_quantize(COST_N_QUANTIZE[c], 0, 2)
-            if c % 2 == 0 and c >= 2:
-                cost_pack("vector", (c - 2) // 2, 0, W)
-            if c in VISITS_PACK_VECTOR:
-                visits_pack("vector", *VISITS_PACK_VECTOR[c], 0, W)
-            for i in ROWS_QUANTIZE.get(c, ()):
-                rows_quantize(i)
+        def output_store(kind, i, t, engine):
+            (contrast_out if kind == "contrast" else account_out)(engine, i, t, out_banks[t % 2])
 
-        def feed_scalar(c):
-            if c % 2 == 1 and c >= 3:
-                s = (c - 3) // 2
-                for h in range(2):
-                    cost_turn(s, h)
-                for h in range(2):
-                    cost_unturn("scalar", s, h)
-            for i in ROWS_TURN.get(c, ()):
-                rows_turn(i)
-            for i in ROWS_TURN.get(c, ()):
-                rows_unturn("scalar", i)
-            if c in VISITS_PACK_SCALAR:
-                visits_pack("scalar", *VISITS_PACK_SCALAR[c], 0, W)
-            for kind, i, t, engine in OUTPUTS.get(c, ()):
-                if kind == "contrast":
-                    contrast_matmul(out_banks[t % 2][:], i, t, 0, W)
-                else:
-                    account_matmul(out_banks[t % 2], i, t, 0, 4)
-                if engine == "scalar":
-                    (contrast_out if kind == "contrast" else account_out)(engine, i, t, out_banks[t % 2])
+        def rows_bank(i):
+            return (turn_banks if i in (4, 5) else out_banks)[i % 2]
 
-        def vector_outputs(c):
-            for kind, i, t, engine in OUTPUTS.get(c, ()):
-                if engine == "vector":
-                    (contrast_out if kind == "contrast" else account_out)(engine, i, t, out_banks[t % 2])
-
-        with tc.manual_schedule(engines={mybir.EngineType.SP}):
+        with tc.manual_schedule():
             load_visits(0, 0)
             load_rows(0, 0, 1)
             load_visits(0, 1)
             load_rows(0, 1, 2)
+            load_visits(1, 0)
+            load_visits(1, 1)
             load_rows(0, 2, 4)
             load_hold(0, 0, 2)
-            load_visits(1, 0)
             load_rows(1, 0, 2)
             load_hold(0, 2, 4)
             load_rows(1, 2, 4)
-            load_visits(1, 1)
-            load_hold(1, 0, 4)
             make_identity(nc, ident[:])
             nc.vector.memset(warm[:, 0:1], 1.0)
             nc.scalar.activation(out=warm[:, 1:2], in_=warm[:, 0:1], func=ACT.Abs_reciprocal_sqrt)
@@ -362,83 +331,152 @@ def tile_jackson_congestion_cost_s8_kernel(
 
             visits_pack("vector", 0, 0, 0, HEAD_SPLIT)
             visits_pack("scalar", 0, 0, HEAD_SPLIT, W)
-            rows_turn(0)
-            rows_unturn("scalar", 0)
-            visits_quantize(0, 0)
-            rows_turn(1)
+            rows_turn(0, rows_bank(0))
+            rows_turn(1, rows_bank(1))
+            rows_unturn("scalar", 0, rows_bank(0))
+            visits_quantize(0, 0, 1)
             visits_pack("vector", 0, 1, 0, W)
-            rows_unturn("scalar", 1)
-            rows_quantize(0)
-            visits_quantize(0, 1)
-            rows_quantize(1)
-            load_visits(2, 0)
-            load_visits(2, 1)
+            rows_quantize(0, 1)
+            visits_quantize(0, 1, 2)
             rho_matmul(0)
+            visits_pack("scalar", 1, 0, 0, W)
+            rows_unturn("vector", 1, rows_bank(1))
+            load_visits(2, 0)
+            load_hold(1, 0, 4)
+            load_visits(2, 1)
+            rows_quantize(1, 1)
             rho_matmul(1)
-            rows_turn(2)
-            rows_turn(3)
-            load_rows(2, 0, 4)
+            visits_pack("vector", 1, 1, 0, W)
+            rows_turn(2, rows_bank(2))
+            rows_turn(3, rows_bank(3))
             load_hold(2, 0, 4)
-            rows_unturn("scalar", 2)
-            rows_unturn("scalar", 3)
-            rows_quantize(2)
-            rows_quantize(3)
+            load_visits(3, 0)
+            load_visits(3, 1)
+            load_rows(2, 0, 4)
+            for s in range(3, 7):
+                load_hold(s, 0, 4)
+            load_c()
+            visits_quantize(1, 0, 2)
 
-            for c in range(16):
+            for c in range(13):
                 for k in (2 * c, 2 * c + 1):
                     square_idle(k)
-                for k in (2 * c, 2 * c + 1):
-                    invert_idle(k)
-                weigh(2 * c)
-                early_vector(c)
-                weigh(2 * c + 1)
-                if c < 15:
-                    rho_matmul(2 * c + 2)
-                    rho_matmul(2 * c + 3)
-                feed_scalar(c)
+                if c >= 2:
+                    cost_unturn("scalar", (c - 2) // 2, c % 2, turn_banks[c % 2])
+                if c == 0:
+                    for i in (2, 3):
+                        rows_unturn("scalar", i, rows_bank(i))
                 if c > 0:
                     finish_pair(c - 1)
-                late_vector(c)
-                vector_outputs(c)
+                if c in ROWS_QUANTIZE:
+                    rows_quantize(ROWS_QUANTIZE[c], 2)
+                invert_idle(c, 0, 2)
+                for kind, i, t, engine in OUTPUTS.get(c - 1, ()):
+                    output_store(kind, i, t, engine)
+                weigh(2 * c)
+                weigh(2 * c + 1)
+                if c == 2:
+                    load_hold(7, 0, 4)
                 if c == 0:
-                    load_visits(3, 0)
-                    load_hold(3, 0, 4)
-                    load_hold(4, 0, 4)
-                if c == 1:
-                    load_visits(3, 1)
-                    for s in range(5, 8):
-                        load_hold(s, 0, 4)
-                    load_c()
+                    rows_quantize(2, 2)
+                    for i in ROWS_UNTURN.get(c, ()):
+                        rows_turn(i, rows_bank(i))
+                rho_matmul(2 * c + 2)
+                rho_matmul(2 * c + 3)
+                if c > 0:
+                    for i in ROWS_UNTURN.get(c, ()):
+                        rows_turn(i, rows_bank(i))
+                    cost_turn((c - 1) // 2, (c - 1) % 2, turn_banks[(c - 1) % 2])
+                for i in ROWS_UNTURN.get(c, ()):
+                    rows_unturn("scalar", i, rows_bank(i))
+                for s, c0, c1 in COST_QUANTIZE_BEFORE.get(c, ()):
+                    cost_quantize(s, c0, c1)
+                if c % 2 == 0 and c >= 2:
+                    cost_pack(COST_PACK.get(c, "vector"), (c - 2) // 2, 0, W)
+                for engine, j, kp, n0, n1 in VISITS_PACK.get(c, ()):
+                    visits_pack(engine, j, kp, n0, n1)
+                if c in VISITS_QUANTIZE:
+                    visits_quantize(VISITS_QUANTIZE[c], 0, 2)
+                for s, c0, c1 in COST_QUANTIZE_AFTER.get(c, ()):
+                    cost_quantize(s, c0, c1)
+                for kind, i, t, engine in OUTPUTS.get(c, ()):
+                    output_matmul(kind, i, t)
 
+            b = banks
+            acc = [b[6], b[7], b[0], b[1]]
+            square_idle(26)
+            square_idle(27)
+            cost_unturn("scalar", 5, 1, b[5])
+            finish_pair(12)
+            contrast_out("vector", 1, 0, b[6])
+            invert_idle(13, 0, 2)
+            contrast_out("scalar", 1, 1, b[7])
+            weigh(26)
+            weigh(27)
+            rho_matmul(28)
+            rho_matmul(29)
+            cost_turn(6, 0, b[4])
+            cost_quantize(5, W, 2 * W)
             for t in range(2, 4):
-                contrast_matmul(out_banks[t % 2][:], 2, t, 0, W)
-            cost_turn(7, 0)
+                contrast_matmul(b[4 + t][:], 1, t, 0, W)
+            square_idle(28)
+            square_idle(29)
+            cost_unturn("scalar", 6, 0, b[4])
+            finish_pair(13)
+            invert_idle(14, 0, 2)
+            contrast_out("scalar", 1, 2, b[6])
+            contrast_out("scalar", 1, 3, b[7])
+            weigh(28)
+            rho_matmul(30)
+            rho_matmul(31)
+            cost_turn(6, 1, b[5])
+            cost_pack("vector", 6, 0, W)
+            weigh(29)
+            cost_quantize(6, 0, W)
+            for t in (2, 0, 1, 3):
+                account_matmul(acc[t], 1, t, 0, 2)
+            square_idle(30)
+            square_idle(31)
+            cost_unturn("scalar", 6, 1, b[5])
+            finish_pair(14)
+            contrast_matmul(b[4][:], 2, 0, 0, W)
+            invert_idle(15, 0, 1)
+            invert_idle(15, 1, 2)
+            weigh(30)
+            weigh(31)
+            cost_turn(7, 0, b[5])
+            contrast_out("scalar", 2, 0, b[4])
+            cost_unturn("scalar", 7, 0, b[5])
             finish_bank(30)
-            cost_unturn("scalar", 7, 0)
-            contrast_out("scalar", 2, 2, out_banks[0])
-            contrast_out("scalar", 2, 3, out_banks[1])
             finish_bank(31)
-            cost_turn(7, 1)
-            for t in range(4):
-                account_matmul(rho_banks[t], 1, t, 0, 3)
+            cost_quantize(6, W, 2 * W)
+            contrast_matmul(b[2][:], 2, 1, 0, W)
+            contrast_matmul(b[3][:], 2, 2, 0, W)
+            contrast_matmul(b[4][:], 2, 3, 0, W)
+            cost_turn(7, 1, b[5])
+            cost_quantize(7, W, W + 256)
+            contrast_out("scalar", 2, 1, b[2])
+            contrast_out("scalar", 2, 2, b[3])
             cost_pack("vector", 7, 0, 256)
-            cost_n_quantize(7, 0, 1)
-            cost_m_quantize(7, 0, 256)
-            cost_unturn("scalar", 7, 1)
+            cost_unturn("scalar", 7, 1, b[5])
             for t in range(2):
-                account_matmul(rho_banks[t], 1, t, 3, 4)
+                account_matmul(acc[t], 1, t, 2, 4)
             cost_pack("vector", 7, 256, W)
-            contrast_half(0, out_banks)
-            for t in range(2):
-                account_out("scalar", 1, t, rho_banks[t])
-            cost_n_quantize(7, 1, 2)
-            cost_m_quantize(7, 256, W)
+            cost_quantize(7, 0, 256)
+            contrast_out("scalar", 2, 3, b[4])
             for t in range(2, 4):
-                account_matmul(rho_banks[t], 1, t, 3, 4)
-            contrast_half(1, turn_banks)
-            contrast_half_out("vector", 0, 0, out_banks[0])
-            contrast_half_out("scalar", 0, 1, out_banks[1])
-            account_out("vector", 1, 2, rho_banks[2])
-            account_out("scalar", 1, 3, rho_banks[3])
-            contrast_half_out("vector", 1, 0, turn_banks[0])
-            contrast_half_out("scalar", 1, 1, turn_banks[1])
+                account_matmul(acc[t], 1, t, 2, 3)
+            contrast_half(0, [b[2], b[3]])
+            cost_quantize(7, W + 256, 2 * W)
+            cost_quantize(7, 256, W)
+            account_out("scalar", 1, 0, acc[0])
+            account_out("vector", 1, 1, acc[1])
+            for t in range(2, 4):
+                account_matmul(acc[t], 1, t, 3, 4)
+            contrast_half(1, [b[4], b[5]])
+            contrast_half_out("scalar", 0, 0, b[2])
+            contrast_half_out("vector", 0, 1, b[3])
+            account_out("scalar", 1, 2, acc[2])
+            account_out("vector", 1, 3, acc[3])
+            contrast_half_out("scalar", 1, 0, b[4])
+            contrast_half_out("vector", 1, 1, b[5])

@@ -19,28 +19,24 @@ MULT = mybir.AluOpType.mult
 P = 128
 PACK = 4
 W = 512
-ORDER = [(0, 0), (1, 0), (0, 1), (0, 2), (0, 3), (1, 1), (1, 2), (1, 3)]
+ORDER = [(g, j) for g in range(2) for j in range(4)]
 HEAD_SPLIT = 336
-VISITS_PACK = {
-    1: [("vector", 2, 0, 0, 512)],
-    3: [("vector", 2, 1, 0, 512)],
-    4: [("scalar", 3, 0, 0, 512)],
-    5: [("vector", 3, 1, 0, 512)],
-}
-COST_PACK = {6: "scalar"}
-VISITS_QUANTIZE = {4: 2, 6: 3}
-ROWS_UNTURN = {0: (4, 5), 1: (6, 7), 3: (8, 9), 5: (10, 11)}
-ROWS_QUANTIZE = {1: 4, 2: 6, 5: 8, 7: 10}
+POOL_COLUMNS = 160
+POOL_SHARE = {9: 160, 11: 384, 13: 288}
+VISITS_PACK = {2: [("vector", 3, 0, 0, 512), ("scalar", 3, 1, 0, 512)]}
+VISITS_QUANTIZE = {3: 3}
+ROWS_UNTURN = {3: (4, 5), 4: (6, 7), 5: (8, 9), 6: (10, 11)}
+ROWS_QUANTIZE = {4: 4, 5: 6, 6: 8, 7: 10}
 COST_QUANTIZE_BEFORE = {
-    3: [(0, 0, 1024)], 5: [(1, 0, 1024)], 8: [(2, 0, 1024)], 9: [(3, 0, 1024)], 10: [(4, 512, 768)],
-    11: [(4, 768, 1024), (4, 0, 512)], 13: [(5, 512, 1024)],
+    3: [(0, 0, 1024)], 5: [(1, 0, 1024)], 7: [(2, 0, 1024)], 8: [(3, 512, 768)],
+    9: [(3, 768, 1024)],
 }
-COST_QUANTIZE_AFTER = {12: [(5, 0, 512)], 14: [(6, 0, 512)]}
+COST_QUANTIZE_AFTER = {10: [(3, 0, 512), (4, 0, 512)], 12: [(4, 512, 1024), (5, 0, 512)]}
 OUTPUTS = {
-    8: [("contrast", 0, 0, "scalar"), ("contrast", 0, 1, "scalar")],
-    9: [("contrast", 0, 2, "scalar"), ("contrast", 0, 3, "scalar")],
-    10: [("account", 0, 0, "scalar"), ("account", 0, 1, "scalar")],
-    11: [("account", 0, 2, "scalar"), ("account", 0, 3, "scalar")],
+    8: [("account", 0, 0, "scalar"), ("account", 0, 1, "scalar")],
+    9: [("account", 0, 2, "scalar"), ("account", 0, 3, "scalar")],
+    10: [("contrast", 0, 0, "vector"), ("contrast", 0, 1, "vector")],
+    11: [("contrast", 0, 2, "scalar"), ("contrast", 0, 3, "scalar")],
     12: [("contrast", 1, 0, "scalar"), ("contrast", 1, 1, "scalar")],
 }
 
@@ -210,11 +206,21 @@ def tile_jackson_congestion_cost_s8_kernel(
                 op=MULT,
             )
 
-        def finish_pair(c):
+        def finish_columns(engine, c, n0, n1):
             t0 = 2 * (c % 2)
-            nc.vector.tensor_tensor(
-                out=cost[(c // 2) % 2][:, t0 : t0 + 2, :], in0=weighted[c % 2][:], in1=inv_idle[c % 3][:], op=MULT
+            engine.tensor_tensor(
+                out=cost[(c // 2) % 2][:, t0 : t0 + 2, n0:n1],
+                in0=weighted[c % 2][:, :, n0:n1],
+                in1=inv_idle[c % 3][:, :, n0:n1],
+                op=MULT,
             )
+
+        def finish_pair(c, share):
+            if share == 0:
+                finish_columns(nc.vector, c, 0, W)
+            else:
+                finish_columns(nc.vector, c, 0, W - share + 16)
+                finish_columns(nc.gpsimd, c, W - share, W)
 
         def finish_bank(k):
             nc.vector.tensor_tensor(
@@ -304,13 +310,13 @@ def tile_jackson_congestion_cost_s8_kernel(
             if kind == "contrast":
                 contrast_matmul(out_banks[t % 2][:], i, t, 0, W)
             else:
-                account_matmul(out_banks[t % 2], i, t, 0, 4)
+                account_matmul(out_banks[t % 2], i, t, 2 if t < 2 else 0, 4)
 
         def output_store(kind, i, t, engine):
             (contrast_out if kind == "contrast" else account_out)(engine, i, t, out_banks[t % 2])
 
         def rows_bank(i):
-            return (turn_banks if i in (4, 5) else out_banks)[i % 2]
+            return out_banks[i % 2]
 
         with tc.manual_schedule():
             load_visits(0, 0)
@@ -321,13 +327,10 @@ def tile_jackson_congestion_cost_s8_kernel(
             load_visits(1, 1)
             load_rows(0, 2, 4)
             load_hold(0, 0, 2)
-            load_rows(1, 0, 2)
-            load_hold(0, 2, 4)
-            load_rows(1, 2, 4)
             make_identity(nc, ident[:])
             nc.vector.memset(warm[:, 0:1], 1.0)
             nc.scalar.activation(out=warm[:, 1:2], in_=warm[:, 0:1], func=ACT.Abs_reciprocal_sqrt)
-            nc.vector.memset(c_plane[:].rearrange("p g n -> p (g n)").bitcast(I32), 0)
+            nc.gpsimd.memset(c_plane[:].rearrange("p g n -> p (g n)").bitcast(I32), 0)
 
             visits_pack("vector", 0, 0, 0, HEAD_SPLIT)
             visits_pack("scalar", 0, 0, HEAD_SPLIT, W)
@@ -342,57 +345,77 @@ def tile_jackson_congestion_cost_s8_kernel(
             visits_pack("scalar", 1, 0, 0, W)
             rows_unturn("vector", 1, rows_bank(1))
             load_visits(2, 0)
-            load_hold(1, 0, 4)
+            load_hold(0, 2, 4)
             load_visits(2, 1)
+            load_hold(1, 0, 4)
             rows_quantize(1, 1)
             rho_matmul(1)
             visits_pack("vector", 1, 1, 0, W)
             rows_turn(2, rows_bank(2))
             rows_turn(3, rows_bank(3))
-            load_hold(2, 0, 4)
             load_visits(3, 0)
             load_visits(3, 1)
+            load_hold(2, 0, 4)
+            load_rows(1, 0, 2)
+            load_rows(1, 2, 4)
+            load_hold(3, 0, 4)
             load_rows(2, 0, 4)
-            for s in range(3, 7):
+            for s in range(4, 7):
                 load_hold(s, 0, 4)
             load_c()
             visits_quantize(1, 0, 2)
 
-            for c in range(13):
+            square_idle(0)
+            square_idle(1)
+            for i in (2, 3):
+                rows_unturn("scalar", i, rows_bank(i))
+            invert_idle(0, 0, 2)
+            weigh(0)
+            weigh(1)
+            rows_quantize(2, 2)
+            rho_matmul(2)
+            rho_matmul(3)
+            visits_pack("scalar", 2, 0, 0, W)
+            finish_pair(0, 0)
+            visits_pack("vector", 2, 1, 0, W)
+            square_idle(2)
+            square_idle(3)
+            invert_idle(1, 0, 2)
+            visits_quantize(2, 0, 2)
+            rho_matmul(4)
+            rho_matmul(5)
+            cost_turn(0, 0, turn_banks[0])
+            weigh(2)
+            weigh(3)
+
+            for c in range(2, 13):
                 for k in (2 * c, 2 * c + 1):
                     square_idle(k)
-                if c >= 2:
-                    cost_unturn("scalar", (c - 2) // 2, c % 2, turn_banks[c % 2])
-                if c == 0:
-                    for i in (2, 3):
-                        rows_unturn("scalar", i, rows_bank(i))
-                if c > 0:
-                    finish_pair(c - 1)
-                if c in ROWS_QUANTIZE:
-                    rows_quantize(ROWS_QUANTIZE[c], 2)
+                cost_unturn("scalar", (c - 2) // 2, c % 2, turn_banks[c % 2])
+                finish_pair(c - 1, POOL_SHARE.get(c, POOL_COLUMNS))
                 invert_idle(c, 0, 2)
-                for kind, i, t, engine in OUTPUTS.get(c - 1, ()):
-                    output_store(kind, i, t, engine)
                 weigh(2 * c)
                 weigh(2 * c + 1)
+                for kind, i, t, engine in OUTPUTS.get(c - 1, ()):
+                    output_store(kind, i, t, engine)
                 if c == 2:
                     load_hold(7, 0, 4)
-                if c == 0:
-                    rows_quantize(2, 2)
-                    for i in ROWS_UNTURN.get(c, ()):
-                        rows_turn(i, rows_bank(i))
                 rho_matmul(2 * c + 2)
                 rho_matmul(2 * c + 3)
-                if c > 0:
-                    for i in ROWS_UNTURN.get(c, ()):
-                        rows_turn(i, rows_bank(i))
-                    cost_turn((c - 1) // 2, (c - 1) % 2, turn_banks[(c - 1) % 2])
+                if c == 7:
+                    for t in range(2):
+                        account_matmul(out_banks[t], 0, t, 0, 2)
+                for i in ROWS_UNTURN.get(c, ()):
+                    rows_turn(i, rows_bank(i))
+                cost_turn((c - 1) // 2, (c - 1) % 2, turn_banks[(c - 1) % 2])
                 for i in ROWS_UNTURN.get(c, ()):
                     rows_unturn("scalar", i, rows_bank(i))
+                if c in ROWS_QUANTIZE:
+                    rows_quantize(ROWS_QUANTIZE[c], 2)
                 for s, c0, c1 in COST_QUANTIZE_BEFORE.get(c, ()):
                     cost_quantize(s, c0, c1)
-                if c % 2 == 0 and c >= 2:
-                    cost_pack(COST_PACK.get(c, "vector"), (c - 2) // 2, 0, W)
+                if c % 2 == 0:
+                    cost_pack("vector", (c - 2) // 2, 0, W)
                 for engine, j, kp, n0, n1 in VISITS_PACK.get(c, ()):
                     visits_pack(engine, j, kp, n0, n1)
                 if c in VISITS_QUANTIZE:
@@ -403,56 +426,57 @@ def tile_jackson_congestion_cost_s8_kernel(
                     output_matmul(kind, i, t)
 
             b = banks
-            acc = [b[6], b[7], b[0], b[1]]
+            acc = [b[4], b[7], b[0], b[1]]
             square_idle(26)
             square_idle(27)
             cost_unturn("scalar", 5, 1, b[5])
-            finish_pair(12)
-            contrast_out("vector", 1, 0, b[6])
+            finish_pair(12, POOL_SHARE[13])
             invert_idle(13, 0, 2)
-            contrast_out("scalar", 1, 1, b[7])
             weigh(26)
             weigh(27)
+            contrast_out("vector", 1, 0, b[6])
+            contrast_out("scalar", 1, 1, b[7])
             rho_matmul(28)
             rho_matmul(29)
-            cost_turn(6, 0, b[4])
+            cost_turn(6, 0, b[5])
             cost_quantize(5, W, 2 * W)
             for t in range(2, 4):
                 contrast_matmul(b[4 + t][:], 1, t, 0, W)
+            account_matmul(acc[0], 1, 0, 0, 2)
             square_idle(28)
             square_idle(29)
-            cost_unturn("scalar", 6, 0, b[4])
-            finish_pair(13)
+            cost_unturn("scalar", 6, 0, b[5])
+            finish_pair(13, POOL_COLUMNS)
             invert_idle(14, 0, 2)
             contrast_out("scalar", 1, 2, b[6])
             contrast_out("scalar", 1, 3, b[7])
             weigh(28)
+            weigh(29)
             rho_matmul(30)
             rho_matmul(31)
             cost_turn(6, 1, b[5])
             cost_pack("vector", 6, 0, W)
-            weigh(29)
-            cost_quantize(6, 0, W)
-            for t in (2, 0, 1, 3):
+            for t in (2, 3, 1):
                 account_matmul(acc[t], 1, t, 0, 2)
             square_idle(30)
             square_idle(31)
             cost_unturn("scalar", 6, 1, b[5])
-            finish_pair(14)
-            contrast_matmul(b[4][:], 2, 0, 0, W)
+            finish_pair(14, 0)
+            cost_quantize(6, 0, W)
+            contrast_matmul(b[6][:], 2, 0, 0, W)
             invert_idle(15, 0, 1)
             invert_idle(15, 1, 2)
             weigh(30)
             weigh(31)
             cost_turn(7, 0, b[5])
-            contrast_out("scalar", 2, 0, b[4])
+            contrast_out("scalar", 2, 0, b[6])
             cost_unturn("scalar", 7, 0, b[5])
             finish_bank(30)
             finish_bank(31)
             cost_quantize(6, W, 2 * W)
             contrast_matmul(b[2][:], 2, 1, 0, W)
             contrast_matmul(b[3][:], 2, 2, 0, W)
-            contrast_matmul(b[4][:], 2, 3, 0, W)
+            contrast_matmul(b[6][:], 2, 3, 0, W)
             cost_turn(7, 1, b[5])
             cost_quantize(7, W, W + 256)
             contrast_out("scalar", 2, 1, b[2])
@@ -463,7 +487,7 @@ def tile_jackson_congestion_cost_s8_kernel(
                 account_matmul(acc[t], 1, t, 2, 4)
             cost_pack("vector", 7, 256, W)
             cost_quantize(7, 0, 256)
-            contrast_out("scalar", 2, 3, b[4])
+            contrast_out("scalar", 2, 3, b[6])
             for t in range(2, 4):
                 account_matmul(acc[t], 1, t, 2, 3)
             contrast_half(0, [b[2], b[3]])
@@ -473,10 +497,10 @@ def tile_jackson_congestion_cost_s8_kernel(
             account_out("vector", 1, 1, acc[1])
             for t in range(2, 4):
                 account_matmul(acc[t], 1, t, 3, 4)
-            contrast_half(1, [b[4], b[5]])
+            contrast_half(1, [b[6], b[5]])
             contrast_half_out("scalar", 0, 0, b[2])
             contrast_half_out("vector", 0, 1, b[3])
             account_out("scalar", 1, 2, acc[2])
             account_out("vector", 1, 3, acc[3])
-            contrast_half_out("scalar", 1, 0, b[4])
+            contrast_half_out("scalar", 1, 0, b[6])
             contrast_half_out("vector", 1, 1, b[5])

@@ -94,10 +94,11 @@ def tile_jackson_congestion_cost_s8_kernel(
         def quantize(codes, scales, packed):
             nc.vector.quantize_mx(out=codes.bitcast(FP8X4), scales=scales, in_=packed)
 
-        def turn(bank, slot, words):
+        def turn(bank, slot, words, sorted_words):
             halves = bank[:].rearrange("p (s u r) -> p s u r", s=2, u=2)
             for u in range(2):
-                nc.tensor.transpose(halves[:, slot, u, :], words[:, u : 256 : 2], ident[:])
+                src = words[:, P * u : P * (u + 1)] if sorted_words else words[:, u : 256 : 2]
+                nc.tensor.transpose(halves[:, slot, u, :], src, ident[:])
 
         def unturn(engine, packed, bank):
             copy_on(
@@ -147,7 +148,7 @@ def tile_jackson_congestion_cost_s8_kernel(
         def rows_turn(i, bank):
             words = rows_raw[(i // 4) % 2][:, i % 4, :].bitcast(F32)
             for kp in range(2):
-                turn(bank, kp, words[:, 256 * kp : 256 * (kp + 1)])
+                turn(bank, kp, words[:, 256 * kp : 256 * (kp + 1)], False)
 
         def rows_unturn(engine, i, bank):
             unturn(engine, rows_packed[(i // 2) % 2][:, i % 2, :, :, :], bank)
@@ -174,6 +175,16 @@ def tile_jackson_congestion_cost_s8_kernel(
         def like(flat, k):
             return flat if k < 30 else flat.rearrange("p (t n) -> p t n", t=2)
 
+        def split(flat, j):
+            if j == 3:
+                return flat
+            return flat.rearrange("p (q u e) -> p u q e", u=2, e=2)
+
+        def plain(flat, j):
+            if j == 3:
+                return flat
+            return flat.rearrange("p (u q e) -> p u q e", u=2, e=2)
+
         def rho_matmul(k):
             g, j = ORDER[k // 4]
             for t, n0, width, col in pieces(k):
@@ -189,8 +200,13 @@ def tile_jackson_congestion_cost_s8_kernel(
                     )
 
         def square_idle(k):
+            j = ORDER[k // 4][1]
             nc.scalar.activation(
-                out=idle_sq[(k // 2) % 2][:, k % 2, :], in_=rho_banks[k % 4][:], func=ACT.Square, bias=1.0, scale=-1.0
+                out=plain(idle_sq[(k // 2) % 2][:, k % 2, :], j),
+                in_=split(rho_banks[k % 4][:], j),
+                func=ACT.Square,
+                bias=1.0,
+                scale=-1.0,
             )
 
         def invert_idle(c, e0, e1):
@@ -199,10 +215,11 @@ def tile_jackson_congestion_cost_s8_kernel(
             )
 
         def weigh(k):
+            j = ORDER[k // 4][1]
             nc.vector.tensor_tensor(
-                out=like(weighted[(k // 2) % 2][:, k % 2, :], k),
-                in0=like(rho_banks[k % 4][:], k),
-                in1=region(hold[(k // 4) % 7], k),
+                out=plain(like(weighted[(k // 2) % 2][:, k % 2, :], k), j),
+                in0=split(like(rho_banks[k % 4][:], k), j),
+                in1=split(region(hold[(k // 4) % 7], k), j),
                 op=MULT,
             )
 
@@ -235,7 +252,7 @@ def tile_jackson_congestion_cost_s8_kernel(
 
         def cost_turn(s, h, bank):
             for slot in range(2):
-                turn(bank, slot, cost[s % 2][:, 2 * h + slot, :].bitcast(F32))
+                turn(bank, slot, cost[s % 2][:, 2 * h + slot, :].bitcast(F32), ORDER[s][1] < 3)
 
         def cost_unturn(engine, s, h, bank):
             packed = cost_packed[s % 2][:, 1, 256 * h : 256 * (h + 1), :]
@@ -280,21 +297,28 @@ def tile_jackson_congestion_cost_s8_kernel(
 
         stored = []
 
-        def store(engine, bank, dst):
+        def store(engine, bank, dst, unsort):
             n = len(stored)
             stored.append(dst)
-            copy_on(engine, result[n % 7][:], bank[:])
+            if unsort:
+                copy_on(
+                    engine,
+                    result[n % 7][:].rearrange("p (q u e) -> p q u e", u=2, e=2),
+                    bank[:].rearrange("p (u q e) -> p q u e", u=2, e=2),
+                )
+            else:
+                copy_on(engine, result[n % 7][:], bank[:])
             nc.sync.dma_start(out=dst, in_=result[n % 7][:])
 
         def contrast_out(engine, j, t, bank):
-            store(engine, bank, contrast_rows[t, :, j * W : (j + 1) * W])
+            store(engine, bank, contrast_rows[t, :, j * W : (j + 1) * W], j < 3)
 
         def account_out(engine, g, t, bank):
-            store(engine, bank, account_rows[g, t])
+            store(engine, bank, account_rows[g, t], False)
 
-        def contrast_half(half, pair):
-            for t in range(4):
-                contrast_matmul(pair[t // 2][:, (t % 2) * 256 : (t % 2 + 1) * 256], 3, t, 256 * half, 256 * (half + 1))
+        def contrast_half(half, h, bank):
+            for e in range(2):
+                contrast_matmul(bank[:, 256 * e : 256 * (e + 1)], 3, 2 * h + e, 256 * half, 256 * (half + 1))
 
         def contrast_half_out(engine, half, h, bank):
             n0 = 3 * W + 256 * half
@@ -319,10 +343,10 @@ def tile_jackson_congestion_cost_s8_kernel(
             return out_banks[i % 2]
 
         with tc.manual_schedule():
-            load_visits(0, 0)
             load_rows(0, 0, 1)
-            load_visits(0, 1)
+            load_visits(0, 0)
             load_rows(0, 1, 2)
+            load_visits(0, 1)
             load_visits(1, 0)
             load_visits(1, 1)
             load_rows(0, 2, 4)
@@ -332,28 +356,28 @@ def tile_jackson_congestion_cost_s8_kernel(
             nc.scalar.activation(out=warm[:, 1:2], in_=warm[:, 0:1], func=ACT.Abs_reciprocal_sqrt)
             nc.gpsimd.memset(c_plane[:].rearrange("p g n -> p (g n)").bitcast(I32), 0)
 
-            visits_pack("vector", 0, 0, 0, HEAD_SPLIT)
-            visits_pack("scalar", 0, 0, HEAD_SPLIT, W)
             rows_turn(0, rows_bank(0))
             rows_turn(1, rows_bank(1))
+            visits_pack("vector", 0, 0, 0, HEAD_SPLIT)
+            visits_pack("scalar", 0, 0, HEAD_SPLIT, W)
             rows_unturn("scalar", 0, rows_bank(0))
+            rows_unturn("scalar", 1, rows_bank(1))
             visits_quantize(0, 0, 1)
             visits_pack("vector", 0, 1, 0, W)
             rows_quantize(0, 1)
             visits_quantize(0, 1, 2)
-            rho_matmul(0)
-            visits_pack("scalar", 1, 0, 0, W)
-            rows_unturn("vector", 1, rows_bank(1))
-            load_visits(2, 0)
-            load_hold(0, 2, 4)
-            load_visits(2, 1)
-            load_hold(1, 0, 4)
             rows_quantize(1, 1)
-            rho_matmul(1)
+            load_visits(2, 0)
+            load_visits(2, 1)
+            load_hold(0, 2, 4)
+            visits_pack("scalar", 1, 0, 0, W)
             visits_pack("vector", 1, 1, 0, W)
+            rho_matmul(0)
+            rho_matmul(1)
             rows_turn(2, rows_bank(2))
             rows_turn(3, rows_bank(3))
             load_visits(3, 0)
+            load_hold(1, 0, 4)
             load_visits(3, 1)
             load_hold(2, 0, 4)
             load_rows(1, 0, 2)
@@ -363,30 +387,32 @@ def tile_jackson_congestion_cost_s8_kernel(
             for s in range(4, 7):
                 load_hold(s, 0, 4)
             load_c()
-            visits_quantize(1, 0, 2)
 
             square_idle(0)
             square_idle(1)
-            for i in (2, 3):
-                rows_unturn("scalar", i, rows_bank(i))
+            rows_unturn("scalar", 2, rows_bank(2))
+            rows_unturn("scalar", 3, rows_bank(3))
             invert_idle(0, 0, 2)
+            visits_quantize(1, 0, 1)
             weigh(0)
             weigh(1)
+            visits_quantize(1, 1, 2)
             rows_quantize(2, 2)
             rho_matmul(2)
             rho_matmul(3)
-            visits_pack("scalar", 2, 0, 0, W)
-            finish_pair(0, 0)
+            visits_pack("scalar", 2, 0, 256, W)
             visits_pack("vector", 2, 1, 0, W)
+            finish_pair(0, 0)
+            visits_pack("vector", 2, 0, 0, 256)
             square_idle(2)
             square_idle(3)
             invert_idle(1, 0, 2)
-            visits_quantize(2, 0, 2)
+            weigh(2)
+            weigh(3)
             rho_matmul(4)
             rho_matmul(5)
             cost_turn(0, 0, turn_banks[0])
-            weigh(2)
-            weigh(3)
+            visits_quantize(2, 0, 2)
 
             for c in range(2, 13):
                 for k in (2 * c, 2 * c + 1):
@@ -428,79 +454,82 @@ def tile_jackson_congestion_cost_s8_kernel(
             b = banks
             acc = [b[4], b[7], b[0], b[1]]
             square_idle(26)
-            square_idle(27)
-            cost_unturn("scalar", 5, 1, b[5])
-            finish_pair(12, POOL_SHARE[13])
-            invert_idle(13, 0, 2)
-            weigh(26)
-            weigh(27)
-            contrast_out("vector", 1, 0, b[6])
-            contrast_out("scalar", 1, 1, b[7])
             rho_matmul(28)
+            finish_pair(12, POOL_SHARE[13])
+            square_idle(27)
+            weigh(26)
+            contrast_out("vector", 1, 0, b[6])
+            cost_unturn("scalar", 5, 1, b[5])
+            weigh(27)
+            invert_idle(13, 0, 2)
+            contrast_out("scalar", 1, 1, b[7])
             rho_matmul(29)
-            cost_turn(6, 0, b[5])
             cost_quantize(5, W, 2 * W)
-            for t in range(2, 4):
-                contrast_matmul(b[4 + t][:], 1, t, 0, W)
-            account_matmul(acc[0], 1, 0, 0, 2)
+            finish_pair(13, POOL_COLUMNS)
             square_idle(28)
             square_idle(29)
-            cost_unturn("scalar", 6, 0, b[5])
-            finish_pair(13, POOL_COLUMNS)
-            invert_idle(14, 0, 2)
-            contrast_out("scalar", 1, 2, b[6])
-            contrast_out("scalar", 1, 3, b[7])
-            weigh(28)
-            weigh(29)
+            cost_turn(6, 0, b[5])
             rho_matmul(30)
+            contrast_matmul(b[6][:], 1, 2, 0, W)
+            contrast_matmul(b[7][:], 1, 3, 0, W)
+            cost_unturn("scalar", 6, 0, b[5])
+            weigh(28)
+            invert_idle(14, 0, 2)
+            weigh(29)
             rho_matmul(31)
             cost_turn(6, 1, b[5])
-            cost_pack("vector", 6, 0, W)
-            for t in (2, 3, 1):
-                account_matmul(acc[t], 1, t, 0, 2)
+            contrast_out("scalar", 1, 3, b[7])
+            account_matmul(acc[3], 1, 3, 0, 2)
             square_idle(30)
-            square_idle(31)
-            cost_unturn("scalar", 6, 1, b[5])
+            cost_pack("vector", 6, 0, W)
             finish_pair(14, 0)
+            account_matmul(acc[0], 1, 0, 0, 2)
+            contrast_out("scalar", 1, 2, b[6])
+            account_matmul(acc[2], 1, 2, 0, 2)
+            cost_unturn("scalar", 6, 1, b[5])
             cost_quantize(6, 0, W)
-            contrast_matmul(b[6][:], 2, 0, 0, W)
+            square_idle(31)
+            weigh(30)
+            account_matmul(acc[1], 1, 1, 0, 2)
             invert_idle(15, 0, 1)
             invert_idle(15, 1, 2)
-            weigh(30)
-            weigh(31)
+            contrast_matmul(b[6][:], 2, 0, 0, W)
             cost_turn(7, 0, b[5])
-            contrast_out("scalar", 2, 0, b[6])
-            cost_unturn("scalar", 7, 0, b[5])
-            finish_bank(30)
-            finish_bank(31)
             cost_quantize(6, W, 2 * W)
+            weigh(31)
             contrast_matmul(b[2][:], 2, 1, 0, W)
+            finish_bank(30)
+            account_matmul(acc[2], 1, 2, 2, 3)
+            contrast_out("scalar", 2, 0, b[6])
+            finish_bank(31)
+            cost_unturn("scalar", 7, 0, b[5])
+            cost_quantize(7, W, W + 256)
+            cost_pack("vector", 7, 0, 256)
             contrast_matmul(b[3][:], 2, 2, 0, W)
             contrast_matmul(b[6][:], 2, 3, 0, W)
-            cost_turn(7, 1, b[5])
-            cost_quantize(7, W, W + 256)
             contrast_out("scalar", 2, 1, b[2])
-            contrast_out("scalar", 2, 2, b[3])
-            cost_pack("vector", 7, 0, 256)
-            cost_unturn("scalar", 7, 1, b[5])
-            for t in range(2):
-                account_matmul(acc[t], 1, t, 2, 4)
+            contrast_out("scalar", 2, 3, b[6])
+            cost_turn(7, 1, b[5])
+            account_matmul(acc[0], 1, 0, 2, 4)
+            account_matmul(acc[1], 1, 1, 2, 4)
             cost_pack("vector", 7, 256, W)
             cost_quantize(7, 0, 256)
-            contrast_out("scalar", 2, 3, b[6])
-            for t in range(2, 4):
-                account_matmul(acc[t], 1, t, 2, 3)
-            contrast_half(0, [b[2], b[3]])
-            cost_quantize(7, W + 256, 2 * W)
-            cost_quantize(7, 256, W)
+            contrast_out("scalar", 2, 2, b[3])
             account_out("scalar", 1, 0, acc[0])
-            account_out("vector", 1, 1, acc[1])
-            for t in range(2, 4):
-                account_matmul(acc[t], 1, t, 3, 4)
-            contrast_half(1, [b[6], b[5]])
+            account_out("scalar", 1, 1, acc[1])
+            contrast_half(0, 0, b[2])
             contrast_half_out("scalar", 0, 0, b[2])
+            cost_unturn("vector", 7, 1, b[5])
+            cost_quantize(7, 256, W)
+            contrast_half(0, 1, b[3])
+            contrast_half(1, 0, b[6])
+            account_matmul(acc[3], 1, 3, 2, 3)
+            cost_quantize(7, W + 256, 2 * W)
+            account_matmul(acc[3], 1, 3, 3, 4)
             contrast_half_out("vector", 0, 1, b[3])
-            account_out("scalar", 1, 2, acc[2])
-            account_out("vector", 1, 3, acc[3])
             contrast_half_out("scalar", 1, 0, b[6])
+            contrast_half(1, 1, b[5])
+            account_matmul(acc[2], 1, 2, 3, 4)
+            account_out("vector", 1, 3, acc[3])
             contrast_half_out("vector", 1, 1, b[5])
+            account_out("scalar", 1, 2, acc[2])

@@ -21,8 +21,9 @@ PACK = 4
 W = 512
 ORDER = [(g, j) for g in range(2) for j in range(4)]
 HEAD_SPLIT = 336
-POOL_COLUMNS = 160
-POOL_SHARE = {9: 160, 11: 384, 13: 288}
+POOL_COLUMNS = 224
+POOL_SHARE = {9: 352, 10: 224, 11: 464, 12: 224, 13: 352}
+ROWS_ON_VECTOR = ()
 VISITS_PACK = {2: [("vector", 3, 0, 0, 512), ("scalar", 3, 1, 0, 512)]}
 VISITS_QUANTIZE = {3: 3}
 ROWS_UNTURN = {3: (4, 5), 4: (6, 7), 5: (8, 9), 6: (10, 11)}
@@ -33,11 +34,11 @@ COST_QUANTIZE_BEFORE = {
 }
 COST_QUANTIZE_AFTER = {10: [(3, 0, 512), (4, 0, 512)], 12: [(4, 512, 1024), (5, 0, 512)]}
 OUTPUTS = {
-    8: [("account", 0, 0, "scalar"), ("account", 0, 1, "scalar")],
+    8: [("account", 0, 0, "vector"), ("account", 0, 1, "scalar")],
     9: [("account", 0, 2, "scalar"), ("account", 0, 3, "scalar")],
     10: [("contrast", 0, 0, "vector"), ("contrast", 0, 1, "vector")],
     11: [("contrast", 0, 2, "scalar"), ("contrast", 0, 3, "scalar")],
-    12: [("contrast", 1, 0, "scalar"), ("contrast", 1, 1, "scalar")],
+    12: [("contrast", 1, 0, "vector"), ("contrast", 1, 1, "scalar")],
 }
 
 
@@ -236,7 +237,8 @@ def tile_jackson_congestion_cost_s8_kernel(
             if share == 0:
                 finish_columns(nc.vector, c, 0, W)
             else:
-                finish_columns(nc.vector, c, 0, W - share + 16)
+                finish_columns(nc.vector, c, W - share, W - share + 16)
+                finish_columns(nc.vector, c, 0, W - share)
                 finish_columns(nc.gpsimd, c, W - share, W)
 
         def finish_bank(k):
@@ -400,10 +402,10 @@ def tile_jackson_congestion_cost_s8_kernel(
             rows_quantize(2, 2)
             rho_matmul(2)
             rho_matmul(3)
-            visits_pack("scalar", 2, 0, 256, W)
+            visits_pack("scalar", 2, 0, 320, W)
             visits_pack("vector", 2, 1, 0, W)
-            finish_pair(0, 0)
-            visits_pack("vector", 2, 0, 0, 256)
+            visits_pack("vector", 2, 0, 0, 320)
+            finish_pair(0, POOL_COLUMNS)
             square_idle(2)
             square_idle(3)
             invert_idle(1, 0, 2)
@@ -424,6 +426,9 @@ def tile_jackson_congestion_cost_s8_kernel(
                 weigh(2 * c + 1)
                 for kind, i, t, engine in OUTPUTS.get(c - 1, ()):
                     output_store(kind, i, t, engine)
+                for i in ROWS_UNTURN.get(c - 1, ()):
+                    if i in ROWS_ON_VECTOR:
+                        rows_unturn("vector", i, rows_bank(i))
                 if c == 2:
                     load_hold(7, 0, 4)
                 rho_matmul(2 * c + 2)
@@ -435,9 +440,8 @@ def tile_jackson_congestion_cost_s8_kernel(
                     rows_turn(i, rows_bank(i))
                 cost_turn((c - 1) // 2, (c - 1) % 2, turn_banks[(c - 1) % 2])
                 for i in ROWS_UNTURN.get(c, ()):
-                    rows_unturn("scalar", i, rows_bank(i))
-                if c in ROWS_QUANTIZE:
-                    rows_quantize(ROWS_QUANTIZE[c], 2)
+                    if i not in ROWS_ON_VECTOR:
+                        rows_unturn("scalar", i, rows_bank(i))
                 for s, c0, c1 in COST_QUANTIZE_BEFORE.get(c, ()):
                     cost_quantize(s, c0, c1)
                 if c % 2 == 0:
@@ -446,6 +450,8 @@ def tile_jackson_congestion_cost_s8_kernel(
                     visits_pack(engine, j, kp, n0, n1)
                 if c in VISITS_QUANTIZE:
                     visits_quantize(VISITS_QUANTIZE[c], 0, 2)
+                if c in ROWS_QUANTIZE:
+                    rows_quantize(ROWS_QUANTIZE[c], 2)
                 for s, c0, c1 in COST_QUANTIZE_AFTER.get(c, ()):
                     cost_quantize(s, c0, c1)
                 for kind, i, t, engine in OUTPUTS.get(c, ()):

from contextlib import ExitStack

import concourse.mybir as mybir
from concourse.masks import make_identity

M, K, N, R, V = 1024, 1024, 2048, 512, 512
FLOPS = 2 * M * K * N + 2 * M * N * R + 2 * V * M * N

F32 = mybir.dt.float32
BF16 = mybir.dt.bfloat16
I32 = mybir.dt.int32
U32 = mybir.dt.uint32
U8 = mybir.dt.uint8
FP8X4 = mybir.dt.float8_e4m3fn_x4
FP4X4 = mybir.dt.float4_e2m1fn_x4
ACT = mybir.ActivationFunctionType
MULT = mybir.AluOpType.mult

P = 128
PACK = 4
W = 512
ORDER = [(g, j) for g in range(2) for j in range(4)]
HEAD_SPLIT = 336
POOL_COLUMNS = 224
POOL_SHARE = {9: 352, 10: 224, 11: 464, 12: 224, 13: 352}
ROWS_ON_VECTOR = ()
VISITS_PACK = {2: [("vector", 3, 0, 0, 512), ("scalar", 3, 1, 0, 512)]}
VISITS_QUANTIZE = {3: 3}
ROWS_UNTURN = {3: (4, 5), 4: (6, 7), 5: (8, 9), 6: (10, 11)}
ROWS_QUANTIZE = {4: 4, 5: 6, 6: 8, 7: 10}
COST_QUANTIZE_BEFORE = {
    3: [(0, 0, 1024)], 5: [(1, 0, 1024)], 7: [(2, 0, 1024)], 8: [(3, 512, 768)],
    9: [(3, 768, 1024)],
}
COST_QUANTIZE_AFTER = {10: [(3, 0, 512), (4, 0, 512)], 12: [(4, 512, 1024), (5, 0, 512)]}
OUTPUTS = {
    8: [("account", 0, 0, "vector"), ("account", 0, 1, "scalar")],
    9: [("account", 0, 2, "scalar"), ("account", 0, 3, "scalar")],
    10: [("contrast", 0, 0, "vector"), ("contrast", 0, 1, "vector")],
    11: [("contrast", 0, 2, "scalar"), ("contrast", 0, 3, "scalar")],
    12: [("contrast", 1, 0, "vector"), ("contrast", 1, 1, "scalar")],
}


def tile_jackson_congestion_cost_s8_kernel(
    tc, arrivals, visits, holding, c_words, c_scales, contrasts, out_0, out_1
):
    nc = tc.nc
    with ExitStack() as ctx:
        sb = ctx.enter_context(tc.tile_pool(name="sb", bufs=1))
        ps = ctx.enter_context(tc.psum_pool(name="ps", bufs=1))

        def tiles(name, count, shape, dtype):
            return [sb.tile(shape, dtype, name="%s%d" % (name, i), align_bytes=64) for i in range(count)]

        banks = [ps.tile([P, W], F32, name="bank%d" % i) for i in range(8)]
        rho_banks, turn_banks, out_banks = banks[0:4], banks[4:6], banks[6:8]

        ident = sb.tile([P, P], F32, name="ident")
        warm = sb.tile([P, 2], F32, name="warm")
        rows_raw = tiles("rows_raw", 2, [P, PACK, K], BF16)
        vis_raw = tiles("vis_raw", 4, [P, PACK, W], BF16)
        hold = tiles("hold", 7, [P, PACK, W], BF16)
        c_codes = sb.tile([P, 4, 2 * R], U8, name="c_codes", align_bytes=64)
        c_plane = sb.tile([P, 4, R], U8, name="c_plane", align_bytes=64)

        vis_packed = tiles("vis_packed", 2, [P, 2, W, PACK], BF16)
        vis_codes = tiles("vis_codes", 4, [P, 2, W], U32)
        vis_scales = tiles("vis_scales", 4, [P, 2, W], U8)
        rows_packed = tiles("rows_packed", 2, [P, 2, 2, P, PACK], BF16)
        rows_codes = tiles("rows_codes", 6, [P, 2, 2, P], U32)
        rows_scales = tiles("rows_scales", 6, [P, 2, 2, P], U8)
        idle_sq = tiles("idle_sq", 2, [P, 2, W], F32)
        inv_idle = tiles("inv_idle", 3, [P, 2, W], F32)
        weighted = tiles("weighted", 2, [P, 2, W], F32)
        cost = tiles("cost", 2, [P, PACK, W], BF16)
        cost_packed = tiles("cost_packed", 2, [P, 2, W, PACK], BF16)
        cost_codes = tiles("cost_codes", 8, [P, 2, W], U32)
        cost_scales = tiles("cost_scales", 8, [P, 2, W], U8)
        result = tiles("result", 7, [P, W], F32)

        def copy_on(engine, out, in_):
            if engine == "scalar":
                nc.scalar.copy(out=out, in_=in_)
            else:
                nc.vector.tensor_copy(out=out, in_=in_)

        def interleave(engine, packed, rows, n0, n1):
            copy_on(
                engine,
                packed[:, n0:n1, :].rearrange("p (c i) t -> p c t i", i=4),
                rows[:, :, n0:n1].rearrange("p t (c i) -> p c t i", i=4),
            )

        def quantize(codes, scales, packed):
            nc.vector.quantize_mx(out=codes.bitcast(FP8X4), scales=scales, in_=packed)

        def turn(bank, slot, words, sorted_words):
            halves = bank[:].rearrange("p (s u r) -> p s u r", s=2, u=2)
            for u in range(2):
                src = words[:, P * u : P * (u + 1)] if sorted_words else words[:, u : 256 : 2]
                nc.tensor.transpose(halves[:, slot, u, :], src, ident[:])

        def unturn(engine, packed, bank):
            copy_on(
                engine,
                packed.rearrange("p s r t -> p s (r t)").bitcast(F32).rearrange("p s (r u) -> p s r u", u=2),
                bank[:].rearrange("p (s u r) -> p s r u", s=2, u=2),
            )

        def load_rows(i, t0, t1):
            src = arrivals[i * W : (i + 1) * W, :] if i < 2 else contrasts
            nc.sync.dma_start(
                out=rows_raw[i % 2][:, t0:t1, :], in_=src.rearrange("(p t) k -> p t k", t=PACK)[:, t0:t1, :]
            )

        def load_visits(j, kp):
            nc.sync.dma_start(
                out=vis_raw[(2 * j + kp) % 4][:],
                in_=visits[kp * W : (kp + 1) * W, j * W : (j + 1) * W].rearrange("(p t) n -> p t n", t=PACK),
            )

        def load_hold(s, t0, t1):
            g, j = ORDER[s]
            nc.sync.dma_start(
                out=hold[s % 7][:, t0:t1, :],
                in_=holding[g * W : (g + 1) * W, j * W : (j + 1) * W].rearrange("(p t) n -> p t n", t=PACK)[:, t0:t1, :],
            )

        def load_c():
            for q in range(4):
                nc.sync.dma_start(
                    out=c_plane[32 * q : 32 * q + 4, :, :].bitcast(I32),
                    in_=c_scales[:, 4 * q : 4 * q + 4, :].rearrange("g r n -> r g n").bitcast(I32),
                )
            nc.sync.dma_start(out=c_codes[:].bitcast(I32), in_=c_words.rearrange("g p b -> p g b").bitcast(I32))

        def visits_pack(engine, j, kp, n0, n1):
            i = 2 * j + kp
            interleave(engine, vis_packed[j % 2][:, kp, :, :], vis_raw[i % 4], n0, n1)

        def visits_quantize(j, kp0, kp1):
            quantize(
                vis_codes[j][:, kp0:kp1, :].rearrange("p s n -> p (s n)"),
                vis_scales[j][:, kp0:kp1, :].rearrange("p s n -> p (s n)"),
                vis_packed[j % 2][:, kp0:kp1, :, :].rearrange("p s n t -> p (s n t)"),
            )

        def rows_turn(i, bank):
            words = rows_raw[(i // 4) % 2][:, i % 4, :].bitcast(F32)
            for kp in range(2):
                turn(bank, kp, words[:, 256 * kp : 256 * (kp + 1)], False)

        def rows_unturn(engine, i, bank):
            unturn(engine, rows_packed[(i // 2) % 2][:, i % 2, :, :, :], bank)

        def rows_quantize(i, count):
            e = slice(i % 2, i % 2 + count)
            quantize(
                rows_codes[i // 2][:, e, :, :].rearrange("p e s r -> p (e s r)"),
                rows_scales[i // 2][:, e, :, :].rearrange("p e s r -> p (e s r)"),
                rows_packed[(i // 2) % 2][:, e, :, :, :].rearrange("p e s r t -> p (e s r t)"),
            )

        def pieces(k):
            s, e = k // 4, k % 4
            if k < 30:
                return [(e, 0, W, 0)]
            return [(t, (k - 30) * 256, 256, (t - 2) * 256) for t in (2, 3)]

        def region(tile, k):
            if k < 30:
                return tile[:, k % 4, :]
            return tile[:, 2:4, (k - 30) * 256 : (k - 29) * 256]

        def like(flat, k):
            return flat if k < 30 else flat.rearrange("p (t n) -> p t n", t=2)

        def split(flat, j):
            if j == 3:
                return flat
            return flat.rearrange("p (q u e) -> p u q e", u=2, e=2)

        def plain(flat, j):
            if j == 3:
                return flat
            return flat.rearrange("p (u q e) -> p u q e", u=2, e=2)

        def rho_matmul(k):
            g, j = ORDER[k // 4]
            for t, n0, width, col in pieces(k):
                for kp in range(2):
                    nc.tensor.matmul_mx(
                        out=rho_banks[k % 4][:, col : col + width],
                        lhsT=rows_codes[2 * g + t // 2][:, t % 2, kp, :].bitcast(FP8X4),
                        lhsT_scale=rows_scales[2 * g + t // 2][:, t % 2, kp, :],
                        rhs=vis_codes[j][:, kp, n0 : n0 + width].bitcast(FP8X4),
                        rhs_scale=vis_scales[j][:, kp, n0 : n0 + width],
                        start=(kp == 0),
                        stop=(kp == 1),
                    )

        def square_idle(k):
            j = ORDER[k // 4][1]
            nc.scalar.activation(
                out=plain(idle_sq[(k // 2) % 2][:, k % 2, :], j),
                in_=split(rho_banks[k % 4][:], j),
                func=ACT.Square,
                bias=1.0,
                scale=-1.0,
            )

        def invert_idle(c, e0, e1):
            nc.scalar.activation(
                out=inv_idle[c % 3][:, e0:e1, :], in_=idle_sq[c % 2][:, e0:e1, :], func=ACT.Abs_reciprocal_sqrt
            )

        def weigh(k):
            j = ORDER[k // 4][1]
            nc.vector.tensor_tensor(
                out=plain(like(weighted[(k // 2) % 2][:, k % 2, :], k), j),
                in0=split(like(rho_banks[k % 4][:], k), j),
                in1=split(region(hold[(k // 4) % 7], k), j),
                op=MULT,
            )

        def finish_columns(engine, c, n0, n1):
            t0 = 2 * (c % 2)
            engine.tensor_tensor(
                out=cost[(c // 2) % 2][:, t0 : t0 + 2, n0:n1],
                in0=weighted[c % 2][:, :, n0:n1],
                in1=inv_idle[c % 3][:, :, n0:n1],
                op=MULT,
            )

        def finish_pair(c, share):
            if share == 0:
                finish_columns(nc.vector, c, 0, W)
            else:
                finish_columns(nc.vector, c, W - share, W - share + 16)
                finish_columns(nc.vector, c, 0, W - share)
                finish_columns(nc.gpsimd, c, W - share, W)

        def finish_bank(k):
            nc.vector.tensor_tensor(
                out=region(cost[(k // 4) % 2], k),
                in0=like(weighted[(k // 2) % 2][:, k % 2, :], k),
                in1=like(inv_idle[(k // 2) % 3][:, k % 2, :], k),
                op=MULT,
            )

        def cost_pack(engine, s, n0, n1):
            interleave(engine, cost_packed[s % 2][:, 0, :, :], cost[s % 2], n0, n1)

        def cost_turn(s, h, bank):
            for slot in range(2):
                turn(bank, slot, cost[s % 2][:, 2 * h + slot, :].bitcast(F32), ORDER[s][1] < 3)

        def cost_unturn(engine, s, h, bank):
            packed = cost_packed[s % 2][:, 1, 256 * h : 256 * (h + 1), :]
            unturn(engine, packed.rearrange("p (s r) t -> p s r t", s=2), bank)

        def cost_quantize(s, c0, c1):
            quantize(
                cost_codes[s][:].rearrange("p a n -> p (a n)")[:, c0:c1],
                cost_scales[s][:].rearrange("p a n -> p (a n)")[:, c0:c1],
                cost_packed[s % 2][:].rearrange("p a n t -> p (a n t)")[:, PACK * c0 : PACK * c1],
            )

        def account_matmul(bank, g, t, j0, j1):
            cols = slice(P * t, P * (t + 1))
            for j in range(j0, j1):
                s = ORDER.index((g, j))
                nc.tensor.matmul_mx(
                    out=bank[:],
                    lhsT=cost_codes[s][:, 1, cols].bitcast(FP8X4),
                    lhsT_scale=cost_scales[s][:, 1, cols],
                    rhs=c_codes[:, j, :].bitcast(FP4X4),
                    rhs_scale=c_plane[:, j, :],
                    start=(j == 0),
                    stop=(j == 3),
                )

        def contrast_matmul(out, j, t, n0, n1):
            for g in range(2):
                s = ORDER.index((g, j))
                nc.tensor.matmul_mx(
                    out=out,
                    lhsT=rows_codes[4 + t // 2][:, t % 2, g, :].bitcast(FP8X4),
                    lhsT_scale=rows_scales[4 + t // 2][:, t % 2, g, :],
                    rhs=cost_codes[s][:, 0, n0:n1].bitcast(FP8X4),
                    rhs_scale=cost_scales[s][:, 0, n0:n1],
                    start=(g == 0),
                    stop=(g == 1),
                )

        account_rows = out_0.rearrange("(g p t) r -> g t p r", g=2, t=PACK)
        contrast_rows = out_1.rearrange("(p t) n -> t p n", t=PACK)

        stored = []

        def store(engine, bank, dst, unsort):
            n = len(stored)
            stored.append(dst)
            if unsort:
                copy_on(
                    engine,
                    result[n % 7][:].rearrange("p (q u e) -> p q u e", u=2, e=2),
                    bank[:].rearrange("p (u q e) -> p q u e", u=2, e=2),
                )
            else:
                copy_on(engine, result[n % 7][:], bank[:])
            nc.sync.dma_start(out=dst, in_=result[n % 7][:])

        def contrast_out(engine, j, t, bank):
            store(engine, bank, contrast_rows[t, :, j * W : (j + 1) * W], j < 3)

        def account_out(engine, g, t, bank):
            store(engine, bank, account_rows[g, t], False)

        def contrast_half(half, h, bank):
            for e in range(2):
                contrast_matmul(bank[:, 256 * e : 256 * (e + 1)], 3, 2 * h + e, 256 * half, 256 * (half + 1))

        def contrast_half_out(engine, half, h, bank):
            n0 = 3 * W + 256 * half
            n = len(stored)
            stored.append(half)
            copy_on(engine, result[n % 7][:], bank[:])
            nc.sync.dma_start(
                out=out_1.rearrange("(p t) n -> p t n", t=PACK)[:, 2 * h : 2 * h + 2, n0 : n0 + 256],
                in_=result[n % 7][:].rearrange("p (t n) -> p t n", t=2),
            )

        def output_matmul(kind, i, t):
            if kind == "contrast":
                contrast_matmul(out_banks[t % 2][:], i, t, 0, W)
            else:
                account_matmul(out_banks[t % 2], i, t, 2 if t < 2 else 0, 4)

        def output_store(kind, i, t, engine):
            (contrast_out if kind == "contrast" else account_out)(engine, i, t, out_banks[t % 2])

        def rows_bank(i):
            return out_banks[i % 2]

        with tc.manual_schedule():
            load_rows(0, 0, 1)
            load_visits(0, 0)
            load_rows(0, 1, 2)
            load_visits(0, 1)
            load_visits(1, 0)
            load_visits(1, 1)
            load_rows(0, 2, 4)
            load_hold(0, 0, 2)
            make_identity(nc, ident[:])
            nc.vector.memset(warm[:, 0:1], 1.0)
            nc.scalar.activation(out=warm[:, 1:2], in_=warm[:, 0:1], func=ACT.Abs_reciprocal_sqrt)
            nc.gpsimd.memset(c_plane[:].rearrange("p g n -> p (g n)").bitcast(I32), 0)

            rows_turn(0, rows_bank(0))
            rows_turn(1, rows_bank(1))
            visits_pack("vector", 0, 0, 0, HEAD_SPLIT)
            visits_pack("scalar", 0, 0, HEAD_SPLIT, W)
            rows_unturn("scalar", 0, rows_bank(0))
            rows_unturn("scalar", 1, rows_bank(1))
            visits_quantize(0, 0, 1)
            visits_pack("vector", 0, 1, 0, W)
            rows_quantize(0, 1)
            visits_quantize(0, 1, 2)
            rows_quantize(1, 1)
            load_visits(2, 0)
            load_visits(2, 1)
            load_hold(0, 2, 4)
            visits_pack("scalar", 1, 0, 0, W)
            visits_pack("vector", 1, 1, 0, W)
            rho_matmul(0)
            rho_matmul(1)
            rows_turn(2, rows_bank(2))
            rows_turn(3, rows_bank(3))
            load_visits(3, 0)
            load_hold(1, 0, 4)
            load_visits(3, 1)
            load_hold(2, 0, 4)
            load_rows(1, 0, 2)
            load_rows(1, 2, 4)
            load_hold(3, 0, 4)
            load_rows(2, 0, 4)
            for s in range(4, 7):
                load_hold(s, 0, 4)
            load_c()

            square_idle(0)
            square_idle(1)
            rows_unturn("scalar", 2, rows_bank(2))
            rows_unturn("scalar", 3, rows_bank(3))
            invert_idle(0, 0, 2)
            visits_quantize(1, 0, 1)
            weigh(0)
            weigh(1)
            visits_quantize(1, 1, 2)
            rows_quantize(2, 2)
            rho_matmul(2)
            rho_matmul(3)
            visits_pack("scalar", 2, 0, 320, W)
            visits_pack("vector", 2, 1, 0, W)
            visits_pack("vector", 2, 0, 0, 320)
            finish_pair(0, POOL_COLUMNS)
            square_idle(2)
            square_idle(3)
            invert_idle(1, 0, 2)
            weigh(2)
            weigh(3)
            rho_matmul(4)
            rho_matmul(5)
            cost_turn(0, 0, turn_banks[0])
            visits_quantize(2, 0, 2)

            for c in range(2, 13):
                for k in (2 * c, 2 * c + 1):
                    square_idle(k)
                cost_unturn("scalar", (c - 2) // 2, c % 2, turn_banks[c % 2])
                finish_pair(c - 1, POOL_SHARE.get(c, POOL_COLUMNS))
                invert_idle(c, 0, 2)
                weigh(2 * c)
                weigh(2 * c + 1)
                for kind, i, t, engine in OUTPUTS.get(c - 1, ()):
                    output_store(kind, i, t, engine)
                for i in ROWS_UNTURN.get(c - 1, ()):
                    if i in ROWS_ON_VECTOR:
                        rows_unturn("vector", i, rows_bank(i))
                if c == 2:
                    load_hold(7, 0, 4)
                rho_matmul(2 * c + 2)
                rho_matmul(2 * c + 3)
                if c == 7:
                    for t in range(2):
                        account_matmul(out_banks[t], 0, t, 0, 2)
                for i in ROWS_UNTURN.get(c, ()):
                    rows_turn(i, rows_bank(i))
                cost_turn((c - 1) // 2, (c - 1) % 2, turn_banks[(c - 1) % 2])
                for i in ROWS_UNTURN.get(c, ()):
                    if i not in ROWS_ON_VECTOR:
                        rows_unturn("scalar", i, rows_bank(i))
                for s, c0, c1 in COST_QUANTIZE_BEFORE.get(c, ()):
                    cost_quantize(s, c0, c1)
                if c % 2 == 0:
                    cost_pack("vector", (c - 2) // 2, 0, W)
                for engine, j, kp, n0, n1 in VISITS_PACK.get(c, ()):
                    visits_pack(engine, j, kp, n0, n1)
                if c in VISITS_QUANTIZE:
                    visits_quantize(VISITS_QUANTIZE[c], 0, 2)
                if c in ROWS_QUANTIZE:
                    rows_quantize(ROWS_QUANTIZE[c], 2)
                for s, c0, c1 in COST_QUANTIZE_AFTER.get(c, ()):
                    cost_quantize(s, c0, c1)
                for kind, i, t, engine in OUTPUTS.get(c, ()):
                    output_matmul(kind, i, t)

            b = banks
            acc = [b[4], b[7], b[0], b[1]]
            square_idle(26)
            rho_matmul(28)
            finish_pair(12, POOL_SHARE[13])
            square_idle(27)
            weigh(26)
            contrast_out("vector", 1, 0, b[6])
            cost_unturn("scalar", 5, 1, b[5])
            weigh(27)
            invert_idle(13, 0, 2)
            contrast_out("scalar", 1, 1, b[7])
            rho_matmul(29)
            cost_quantize(5, W, 2 * W)
            finish_pair(13, POOL_COLUMNS)
            square_idle(28)
            square_idle(29)
            cost_turn(6, 0, b[5])
            rho_matmul(30)
            contrast_matmul(b[6][:], 1, 2, 0, W)
            contrast_matmul(b[7][:], 1, 3, 0, W)
            cost_unturn("scalar", 6, 0, b[5])
            weigh(28)
            invert_idle(14, 0, 2)
            weigh(29)
            rho_matmul(31)
            cost_turn(6, 1, b[5])
            contrast_out("scalar", 1, 3, b[7])
            account_matmul(acc[3], 1, 3, 0, 2)
            square_idle(30)
            cost_pack("vector", 6, 0, W)
            finish_pair(14, 0)
            account_matmul(acc[0], 1, 0, 0, 2)
            contrast_out("scalar", 1, 2, b[6])
            account_matmul(acc[2], 1, 2, 0, 2)
            cost_unturn("scalar", 6, 1, b[5])
            cost_quantize(6, 0, W)
            square_idle(31)
            weigh(30)
            account_matmul(acc[1], 1, 1, 0, 2)
            invert_idle(15, 0, 1)
            invert_idle(15, 1, 2)
            contrast_matmul(b[6][:], 2, 0, 0, W)
            cost_turn(7, 0, b[5])
            cost_quantize(6, W, 2 * W)
            weigh(31)
            contrast_matmul(b[2][:], 2, 1, 0, W)
            finish_bank(30)
            account_matmul(acc[2], 1, 2, 2, 3)
            contrast_out("scalar", 2, 0, b[6])
            finish_bank(31)
            cost_unturn("scalar", 7, 0, b[5])
            cost_quantize(7, W, W + 256)
            cost_pack("vector", 7, 0, 256)
            contrast_matmul(b[3][:], 2, 2, 0, W)
            contrast_matmul(b[6][:], 2, 3, 0, W)
            contrast_out("scalar", 2, 1, b[2])
            contrast_out("scalar", 2, 3, b[6])
            cost_turn(7, 1, b[5])
            account_matmul(acc[0], 1, 0, 2, 4)
            account_matmul(acc[1], 1, 1, 2, 4)
            cost_pack("vector", 7, 256, W)
            cost_quantize(7, 0, 256)
            contrast_out("scalar", 2, 2, b[3])
            account_out("scalar", 1, 0, acc[0])
            account_out("scalar", 1, 1, acc[1])
            contrast_half(0, 0, b[2])
            contrast_half_out("scalar", 0, 0, b[2])
            cost_unturn("vector", 7, 1, b[5])
            cost_quantize(7, 256, W)
            contrast_half(0, 1, b[3])
            contrast_half(1, 0, b[6])
            account_matmul(acc[3], 1, 3, 2, 3)
            cost_quantize(7, W + 256, 2 * W)
            account_matmul(acc[3], 1, 3, 3, 4)
            contrast_half_out("vector", 0, 1, b[3])
            contrast_half_out("scalar", 1, 0, b[6])
            contrast_half(1, 1, b[5])
            account_matmul(acc[2], 1, 2, 3, 4)
            account_out("vector", 1, 3, acc[3])
            contrast_half_out("vector", 1, 1, b[5])
            account_out("scalar", 1, 2, acc[2])
